import numpy as np
import ml_dtypes


def mxq(x, axis, fmt="e4m3"):
    dtype, down = {"e4m3": (ml_dtypes.float8_e4m3fn, 7), "e5m2": (ml_dtypes.float8_e5m2, 14)}[fmt]
    v = np.moveaxis(np.asarray(x, np.float32).astype(ml_dtypes.bfloat16).astype(np.float64), axis, -1)
    blocks = v.reshape(v.shape[:-1] + (-1, 32))
    amax = np.abs(blocks).max(-1, keepdims=True)
    byte = np.maximum(np.where(amax > 0, np.frexp(amax)[1] - 1 + 127, 0) - down, 1)
    scale = np.exp2(byte - 127.0)
    codes = (blocks / scale).astype(np.float32).astype(dtype).astype(np.float64)
    return np.moveaxis((codes * scale).reshape(v.shape), -1, axis)


WIDE = False


def mx_kscale(k):
    if not WIDE:
        return np.ones(k)
    levels = np.array([10, -10, 5, -5, 0])
    if k % 512:
        return np.exp2(np.random.permutation(np.resize(levels, k // 32))).repeat(32)
    a = np.empty((k // 512, 16))
    for p in range(k // 512):
        a[p, :8] = np.random.permutation(np.resize(levels, 8))
        for g in range(8):
            far = levels[np.abs(levels - a[p, g]) >= 10]
            a[p, g + 8] = far[np.random.randint(len(far))]
    return np.exp2(a.ravel()).repeat(32)


def f64(x):
    return np.asarray(x).astype(np.float64)


def striped(idx):
    return np.tile(idx.reshape(-1, 16).T, (8, 1)).astype(np.uint16)


def unstriped(offs):
    return offs[:16].T.reshape(-1).astype(np.int64)


E2M1 = np.array([0.0, 0.5, 1.0, 1.5, 2.0, 3.0, 4.0, 6.0, -0.0, -0.5, -1.0, -1.5, -2.0, -3.0, -4.0, -6.0])


def pack_weight(w, fmt):
    k, n = w.shape
    w = f64(np.asarray(w, np.float32).astype(ml_dtypes.bfloat16)).reshape(k // 32, 32, n)
    amax = np.abs(w).max(1)
    if fmt == "e4m3":
        byte = np.frexp(amax)[1] - 1 + 127 - 7
    else:
        mant, ex = np.frexp(amax / 6.0)
        byte = np.where(mant > 0.5, ex, ex - 1) + 127
    byte = np.clip(np.where(amax > 0, byte, 1), 1, 254)
    scaled = (w * np.exp2(127.0 - byte)[:, None, :]).reshape(k, n).astype(np.float32)
    by_word = np.ascontiguousarray(scaled.reshape(k // 512, 128, 4, n).transpose(0, 1, 3, 2))
    if fmt == "e4m3":
        words = by_word.astype(ml_dtypes.float8_e4m3fn).view(np.uint8)
    else:
        c = by_word.astype(ml_dtypes.float4_e2m1fn).view(np.uint8) & 0xF
        words = (c[..., 0::2] | (c[..., 1::2] << 4)).reshape(k // 512, 128, 2 * n)
    return np.ascontiguousarray(words), np.ascontiguousarray(byte.astype(np.uint8).reshape(k // 512, 16, n))


def unpack_weight(words, scales, fmt):
    g, _, n = scales.shape
    words = np.ascontiguousarray(words).reshape(g, 128, n, -1)
    if fmt == "e4m3":
        vals = words.view(ml_dtypes.float8_e4m3fn).astype(np.float64)
    else:
        nib = np.empty((g, 128, n, 4), np.uint8)
        nib[..., 0::2] = words & 0xF
        nib[..., 1::2] = words >> 4
        vals = E2M1[nib]
    vals = vals * np.repeat(np.exp2(scales.astype(np.float64) - 127.0), 8, axis=1)[..., None]
    return vals.transpose(0, 1, 3, 2).reshape(g * 512, n)


def sigmoid(v):
    return 1.0 / (1.0 + np.exp(-np.maximum(v, -700.0)))


K, T, E, C, H, N = 512, 1536, 6, 128, 512, 256


def by_expert(wq, xq):
    return np.concatenate([wq[e].T @ xq[:, e * C:(e + 1) * C] for e in range(E)], axis=1)


def setup_inputs():
    n = np.random.standard_normal
    s = mx_kscale(K)[:, None]
    u = mx_kscale(H)
    w1 = [pack_weight(m, "e2m1") for m in n((E, K, H)) / np.sqrt(K) / s[None]]
    w3 = [pack_weight(m, "e2m1") for m in n((E, K, H)) / np.sqrt(K) / s[None] * u[None, None, :]]
    w2 = [pack_weight(m, "e2m1") for m in n((E, H, N)) / np.sqrt(H) / u[None, :, None]]
    return {
        "xT": (n((K, T)) * s).astype(np.float32),
        "w1_words": np.stack([m[0] for m in w1]),
        "w1_scales": np.stack([m[1] for m in w1]),
        "w3_words": np.stack([m[0] for m in w3]),
        "w3_scales": np.stack([m[1] for m in w3]),
        "w2_words": np.stack([m[0] for m in w2]),
        "w2_scales": np.stack([m[1] for m in w2]),
        "gate": np.tile(np.random.uniform(0.2, 1.0, E * C), (N, 1)).astype(np.float32),
        "offs": striped(np.random.permutation(T)[:E * C]),
        "dst": striped(np.random.permutation(T)[:E * C]),
    }


def reference(xT, w1_words, w1_scales, w3_words, w3_scales, w2_words, w2_scales, gate, offs, dst):
    idx = unstriped(offs)
    w1 = np.stack([unpack_weight(w1_words[e], w1_scales[e], "e2m1") for e in range(E)])
    w3 = np.stack([unpack_weight(w3_words[e], w3_scales[e], "e2m1") for e in range(E)])
    w2 = np.stack([unpack_weight(w2_words[e], w2_scales[e], "e2m1") for e in range(E)])
    xq = mxq(f64(xT)[:, idx], 0, "e4m3")
    h = sigmoid(by_expert(w1, xq))
    h = h * by_expert(w3, xq)
    y = by_expert(w2, mxq(h, 0, "e4m3"))
    out = np.zeros((N, T))
    out[:, unstriped(dst)] = f64(gate) * y
    return out

@@ -1,0 +1,258 @@
+from contextlib import ExitStack
+
+import concourse.mybir as mybir
+from concourse.masks import make_identity
+
+K, T, E, C, H, N = 512, 1536, 6, 128, 512, 256
+FLOPS = 2 * E * C * (2 * K * H + H * N)
+
+F32 = mybir.dt.float32
+BF16 = mybir.dt.bfloat16
+I32 = mybir.dt.int32
+U32 = mybir.dt.uint32
+U16 = mybir.dt.uint16
+U8 = mybir.dt.uint8
+FP8X4 = mybir.dt.float8_e4m3fn_x4
+FP4X4 = mybir.dt.float4_e2m1fn_x4
+ACT = mybir.ActivationFunctionType
+MULT = mybir.AluOpType.mult
+
+P = 128
+G = 3
+GS = 2 * C
+GO = GS // 16
+
+
+def tile_moe_two_glu_sigmoid_kernel(
+    tc, xT, w1_words, w1_scales, w3_words, w3_scales, w2_words, w2_scales, gate, offs, dst, out
+):
+    nc = tc.nc
+    with ExitStack() as ctx:
+        keep = ctx.enter_context(tc.tile_pool(name="keep", bufs=1))
+        work = ctx.enter_context(tc.tile_pool(name="work", bufs=3))
+        psum = ctx.enter_context(tc.psum_pool(name="psum", bufs=2))
+
+        offs_sb = keep.tile([P, E * C // 16], U16, name="offs_sb")
+        dst_sb = keep.tile([P, E * C // 16], U16, name="dst_sb")
+        warm = keep.tile([P, 1], F32, name="warm")
+        ident = keep.tile([P, P], F32, name="ident")
+        planes = [keep.tile([P, T], F32, name=f"plane{j}") for j in range(4)]
+        w1_sb = keep.tile([P, E, 2 * H], U8, name="w1_sb", align_bytes=64)
+        w3_sb = keep.tile([P, E, 2 * H], U8, name="w3_sb", align_bytes=64)
+        w2_sb = keep.tile([P, E, 2 * N], U8, name="w2_sb", align_bytes=64)
+        s1_sb = keep.tile([P, E, H], U8, name="s1_sb", align_bytes=64)
+        s3_sb = keep.tile([P, E, H], U8, name="s3_sb", align_bytes=64)
+        s2_sb = keep.tile([P, E, N], U8, name="s2_sb", align_bytes=64)
+        gate_sb = keep.tile([P, 2, E * C], F32, name="gate_sb")
+        wins = [keep.tile([P, T], F32, name=f"win{h}") for h in range(2)]
+        p01 = keep.tile([P, 2, E * C], F32, name="p01")
+        p23 = [keep.tile([P, 2, GS], F32, name=f"p23_{g}") for g in range(G)]
+        x4 = [keep.tile([P, GS, 4], BF16, name=f"x4_{g}", align_bytes=64) for g in range(G)]
+        xq = [keep.tile([P, GS], U32, name=f"xq_{g}", align_bytes=64) for g in range(G)]
+        xs = [keep.tile([P, GS], U8, name=f"xs_{g}", align_bytes=64) for g in range(G)]
+
+        nc.sync.dma_start(offs_sb[:], offs)
+        xv = xT.rearrange("(p j) t -> p j t", j=4)
+        for j in range(4):
+            nc.sync.dma_start(out=planes[j][:], in_=xv[:, j, :])
+
+        nc.vector.memset(warm[:], 0.0)
+        nc.scalar.activation(warm[:], warm[:], ACT.Sigmoid)
+        for t in (s1_sb, s3_sb, s2_sb):
+            nc.vector.memset(t[:].rearrange("p e i -> p (e i)").bitcast(I32), 0)
+        for w in wins:
+            nc.gpsimd.memset(w[:], 0.0)
+        make_identity(nc, ident[:])
+
+        def load_scales(tile, dram):
+            flat = tile[:].rearrange("p e i -> p (e i)").bitcast(I32)
+            w = tile.shape[2] // 4
+            for q in range(4):
+                nc.sync.dma_start(
+                    out=flat[32 * q : 32 * q + 4, :].rearrange("r (e i) -> r e i", i=w),
+                    in_=dram[:, 0, 4 * q : 4 * q + 4, :].rearrange("e r i -> r e i").bitcast(I32),
+                )
+
+        def load_words(tile, dram, e0, e1):
+            nc.sync.dma_start(
+                out=tile[:, e0:e1, :].bitcast(I32),
+                in_=dram[e0:e1, 0, :, :].rearrange("e p b -> p e b").bitcast(I32),
+            )
+
+        load_words(w1_sb, w1_words, 0, 2)
+        load_scales(s1_sb, w1_scales)
+        load_words(w3_sb, w3_words, 0, 2)
+        load_scales(s3_sb, w3_scales)
+        load_words(w1_sb, w1_words, 2, 4)
+        load_words(w3_sb, w3_words, 2, 4)
+        load_words(w1_sb, w1_words, 4, 6)
+        load_words(w3_sb, w3_words, 4, 6)
+        load_scales(s2_sb, w2_scales)
+        load_words(w2_sb, w2_words, 0, 6)
+        nc.sync.dma_start(dst_sb[:], dst)
+        nc.sync.dma_start(out=gate_sb[:], in_=gate.rearrange("(h p) j -> p h j", p=P))
+
+        def gather(j, g):
+            nc.vector.tensor_copy(p23[g][:, j - 2, :], planes[j][:].indirect(offs_sb[:, GO * g : GO * (g + 1)]))
+
+        def precast(g):
+            nc.scalar.copy(x4[g][:, :, 0:2], p01[:, :, GS * g : GS * (g + 1)].rearrange("p t c -> p c t"))
+
+        def cast(g, eng):
+            dst_ap, src_ap = x4[g][:, :, 2:4], p23[g][:].rearrange("p t c -> p c t")
+            if eng == "V":
+                nc.vector.tensor_copy(dst_ap, src_ap)
+            elif eng == "G":
+                nc.gpsimd.tensor_scalar(dst_ap, src_ap, 1.0, 0.0, MULT, mybir.AluOpType.add)
+            else:
+                nc.scalar.copy(dst_ap, src_ap)
+
+        def quant(g):
+            nc.vector.quantize_mx(
+                out=xq[g][:].bitcast(FP8X4), scales=xs[g][:], in_=x4[g][:].rearrange("p c t -> p (c t)")
+            )
+
+        acc, sig, hid, turned, h4s, hqs, ys, ysb = {}, {}, {}, {}, {}, {}, {}, {}
+
+        def first(e, name, w, s):
+            g, c = divmod(e, 2)
+            cols = slice(C * c, C * (c + 1))
+            t = psum.tile([P, H], F32, name=name)
+            nc.tensor.matmul_mx(
+                out=t[:],
+                lhsT=xq[g][:, cols].bitcast(FP8X4),
+                lhsT_scale=xs[g][:, cols],
+                rhs=w[:, e, :].bitcast(FP4X4),
+                rhs_scale=s[:, e, :],
+                start=True,
+                stop=True,
+            )
+            acc[name, e] = t
+
+        def sigm(e):
+            sg = work.tile([P, H], F32, name="sg")
+            nc.scalar.activation(sg[:], acc["a", e][:], ACT.Sigmoid)
+            sig[e] = sg
+
+        def mul(e):
+            h = keep.tile([P, H], BF16, name=f"h{e}")
+            nc.vector.tensor_tensor(h[:], acc["b", e][:], sig[e][:], MULT)
+            hid[e] = h
+
+        def turn(g):
+            tp = psum.tile([P, 2, 2, C], F32, name="tp")
+            for c in range(2):
+                words = hid[2 * g + c][:].bitcast(F32)
+                for u in range(2):
+                    nc.tensor.transpose(tp[:, c, u, :], words[:, u::2], ident[:])
+            turned[g] = tp
+
+        def evt(g):
+            h4 = work.tile([P, 2, C, 4], BF16, name="h4", align_bytes=64)
+            h4w = h4[:].rearrange("p e c t -> p (e c t)")
+            nc.scalar.copy(
+                h4w.bitcast(F32).rearrange("p (e c u) -> p e c u", e=2, u=2),
+                turned[g][:].rearrange("p e u c -> p e c u"),
+            )
+            h4s[g] = h4w
+
+        def hquant(g):
+            hq = work.tile([P, GS], U32, name="hq", align_bytes=64)
+            hsc = work.tile([P, GS], U8, name="hsc", align_bytes=64)
+            nc.vector.quantize_mx(out=hq[:].bitcast(FP8X4), scales=hsc[:], in_=h4s[g])
+            hqs[g] = (hq, hsc)
+
+        def second(g):
+            hq, hsc = hqs[g]
+            y = psum.tile([P, 2, GS], F32, name="y")
+            for c in range(2):
+                cols = slice(C * c, C * (c + 1))
+                for n in range(2):
+                    nc.tensor.matmul_mx(
+                        out=y[:, n, cols],
+                        lhsT=w2_sb[:, 2 * g + c, 2 * P * n : 2 * P * (n + 1)].bitcast(FP4X4),
+                        lhsT_scale=s2_sb[:, 2 * g + c, P * n : P * (n + 1)],
+                        rhs=hq[:, cols].bitcast(FP8X4),
+                        rhs_scale=hsc[:, cols],
+                        start=True,
+                        stop=True,
+                    )
+            ys[g] = y
+
+        def evy(g):
+            y_sb = work.tile([P, 2, GS], F32, name="y_sb")
+            nc.scalar.copy(y_sb[:], ys[g][:])
+            ysb[g] = y_sb
+
+        def scatter(g, n):
+            nc.vector.tensor_tensor(
+                wins[n][:].indirect(dst_sb[:, GO * g : GO * (g + 1)]),
+                ysb[g][:, n, :],
+                gate_sb[:, n, GS * g : GS * (g + 1)],
+                MULT,
+            )
+            if g == G - 1:
+                nc.sync.dma_start(out[P * n : P * (n + 1), :], wins[n][:])
+
+        nc.vector.tensor_copy(p01[:, 0, :], planes[0][:].indirect(offs_sb[:]))
+        nc.vector.tensor_copy(p01[:, 1, :], planes[1][:].indirect(offs_sb[:]))
+        precast(0)
+        precast(1)
+        precast(2)
+        gather(2, 0)
+        gather(2, 1)
+        gather(3, 0)
+        cast(0, "S")
+        gather(3, 1)
+        cast(1, "S")
+        gather(3, 2)
+        quant(0)
+        gather(2, 2)
+        quant(1)
+        first(0, "a", w1_sb, s1_sb)
+        first(1, "a", w1_sb, s1_sb)
+        first(0, "b", w3_sb, s3_sb)
+        first(1, "b", w3_sb, s3_sb)
+        sigm(0)
+        sigm(1)
+        mul(0)
+        mul(1)
+        first(2, "a", w1_sb, s1_sb)
+        sigm(2)
+        cast(2, "S")
+        quant(2)
+        first(3, "a", w1_sb, s1_sb)
+        first(2, "b", w3_sb, s3_sb)
+        first(3, "b", w3_sb, s3_sb)
+        sigm(3)
+        mul(2)
+        mul(3)
+        turn(0)
+        evt(0)
+        hquant(0)
+        first(4, "a", w1_sb, s1_sb)
+        first(5, "a", w1_sb, s1_sb)
+        first(4, "b", w3_sb, s3_sb)
+        first(5, "b", w3_sb, s3_sb)
+        sigm(4)
+        sigm(5)
+        mul(4)
+        mul(5)
+        second(0)
+        evy(0)
+        turn(1)
+        evt(1)
+        turn(2)
+        evt(2)
+        scatter(0, 0)
+        hquant(1)
+        hquant(2)
+        second(1)
+        second(2)
+        evy(1)
+        evy(2)
+        scatter(0, 1)
+        scatter(1, 0)
+        scatter(2, 0)
+        scatter(1, 1)
+        scatter(2, 1)

@@ -30,21 +30,19 @@ def tile_moe_two_glu_sigmoid_kernel(
     with ExitStack() as ctx:
         keep = ctx.enter_context(tc.tile_pool(name="keep", bufs=1))
         work = ctx.enter_context(tc.tile_pool(name="work", bufs=3))
-        psum = ctx.enter_context(tc.psum_pool(name="psum", bufs=2))
+        psum = ctx.enter_context(tc.psum_pool(name="psum", bufs=8))
 
         offs_sb = keep.tile([P, E * C // 16], U16, name="offs_sb")
         dst_sb = keep.tile([P, E * C // 16], U16, name="dst_sb")
         warm = keep.tile([P, 1], F32, name="warm")
         ident = keep.tile([P, P], F32, name="ident")
-        planes = [keep.tile([P, T], F32, name=f"plane{j}") for j in range(4)]
-        w1_sb = keep.tile([P, E, 2 * H], U8, name="w1_sb", align_bytes=64)
-        w3_sb = keep.tile([P, E, 2 * H], U8, name="w3_sb", align_bytes=64)
-        w2_sb = keep.tile([P, E, 2 * N], U8, name="w2_sb", align_bytes=64)
+        planes = [keep.tile([P, T], F32, name=f"plane{j}", align_bytes=64) for j in range(4)]
         s1_sb = keep.tile([P, E, H], U8, name="s1_sb", align_bytes=64)
         s3_sb = keep.tile([P, E, H], U8, name="s3_sb", align_bytes=64)
         s2_sb = keep.tile([P, E, N], U8, name="s2_sb", align_bytes=64)
-        gate_sb = keep.tile([P, 2, E * C], F32, name="gate_sb")
-        wins = [keep.tile([P, T], F32, name=f"win{h}") for h in range(2)]
+        wins = [keep.tile([P, T], F32, name=f"win{h}", align_bytes=64) for h in range(2)]
+        zq = keep.tile([P, H], U32, name="zq", align_bytes=64)
+        zs = keep.tile([P, H], U8, name="zs", align_bytes=64)
         p01 = keep.tile([P, 2, E * C], F32, name="p01")
         p23 = [keep.tile([P, 2, GS], F32, name=f"p23_{g}") for g in range(G)]
         x4 = [keep.tile([P, GS, 4], BF16, name=f"x4_{g}", align_bytes=64) for g in range(G)]
@@ -52,6 +50,7 @@ def tile_moe_two_glu_sigmoid_kernel(
         xs = [keep.tile([P, GS], U8, name=f"xs_{g}", align_bytes=64) for g in range(G)]
 
         nc.sync.dma_start(offs_sb[:], offs)
+        nc.sync.dma_start(dst_sb[:], dst)
         xv = xT.rearrange("(p j) t -> p j t", j=4)
         for j in range(4):
             nc.sync.dma_start(out=planes[j][:], in_=xv[:, j, :])
@@ -63,111 +62,85 @@ def tile_moe_two_glu_sigmoid_kernel(
         for w in wins:
             nc.gpsimd.memset(w[:], 0.0)
         make_identity(nc, ident[:])
+        nc.vector.quantize_mx(out=zq[:].bitcast(FP8X4), scales=zs[:], in_=wins[0][:].bitcast(BF16)[:, 0 : 4 * H])
 
         def load_scales(tile, dram):
             flat = tile[:].rearrange("p e i -> p (e i)").bitcast(I32)
             w = tile.shape[2] // 4
-            for q in range(4):
+            for r in range(4):
                 nc.sync.dma_start(
-                    out=flat[32 * q : 32 * q + 4, :].rearrange("r (e i) -> r e i", i=w),
-                    in_=dram[:, 0, 4 * q : 4 * q + 4, :].rearrange("e r i -> r e i").bitcast(I32),
+                    out=flat[r:P:32, :].rearrange("q (e i) -> q e i", i=w),
+                    in_=dram[:, 0, r:16:4, :].rearrange("e q i -> q e i").bitcast(I32),
                 )
 
-        def load_words(tile, dram, e0, e1):
+        def load_words(view, dram, e0, e1):
             nc.sync.dma_start(
-                out=tile[:, e0:e1, :].bitcast(I32),
+                out=view.bitcast(I32),
                 in_=dram[e0:e1, 0, :, :].rearrange("e p b -> p e b").bitcast(I32),
             )
 
-        load_words(w1_sb, w1_words, 0, 2)
-        load_scales(s1_sb, w1_scales)
-        load_words(w3_sb, w3_words, 0, 2)
-        load_scales(s3_sb, w3_scales)
-        load_words(w1_sb, w1_words, 2, 4)
-        load_words(w3_sb, w3_words, 2, 4)
-        load_words(w1_sb, w1_words, 4, 6)
-        load_words(w3_sb, w3_words, 4, 6)
-        load_scales(s2_sb, w2_scales)
-        load_words(w2_sb, w2_words, 0, 6)
-        nc.sync.dma_start(dst_sb[:], dst)
-        nc.sync.dma_start(out=gate_sb[:], in_=gate.rearrange("(h p) j -> p h j", p=P))
-
-        def gather(j, g):
-            nc.vector.tensor_copy(p23[g][:, j - 2, :], planes[j][:].indirect(offs_sb[:, GO * g : GO * (g + 1)]))
-
-        def precast(g):
-            nc.scalar.copy(x4[g][:, :, 0:2], p01[:, :, GS * g : GS * (g + 1)].rearrange("p t c -> p c t"))
-
-        def cast(g, eng):
-            dst_ap, src_ap = x4[g][:, :, 2:4], p23[g][:].rearrange("p t c -> p c t")
-            if eng == "V":
-                nc.vector.tensor_copy(dst_ap, src_ap)
-            elif eng == "G":
-                nc.gpsimd.tensor_scalar(dst_ap, src_ap, 1.0, 0.0, MULT, mybir.AluOpType.add)
-            else:
-                nc.scalar.copy(dst_ap, src_ap)
+        def slots(lst, g):
+            return lst[:, GO * g : GO * (g + 1)]
 
         def quant(g):
             nc.vector.quantize_mx(
                 out=xq[g][:].bitcast(FP8X4), scales=xs[g][:], in_=x4[g][:].rearrange("p c t -> p (c t)")
             )
 
-        acc, sig, hid, turned, h4s, hqs, ys, ysb = {}, {}, {}, {}, {}, {}, {}, {}
+        hid, hqs, ys = {}, {}, {}
 
-        def first(e, name, w, s):
+        def first(e, m, s):
             g, c = divmod(e, 2)
             cols = slice(C * c, C * (c + 1))
-            t = psum.tile([P, H], F32, name=name)
+            t = psum.tile([P, H], F32, name="bank")
             nc.tensor.matmul_mx(
                 out=t[:],
                 lhsT=xq[g][:, cols].bitcast(FP8X4),
                 lhsT_scale=xs[g][:, cols],
-                rhs=w[:, e, :].bitcast(FP4X4),
+                rhs=w13[g][m][:, c, :].bitcast(FP4X4),
                 rhs_scale=s[:, e, :],
                 start=True,
                 stop=True,
             )
-            acc[name, e] = t
+            return t
 
-        def sigm(e):
-            sg = work.tile([P, H], F32, name="sg")
-            nc.scalar.activation(sg[:], acc["a", e][:], ACT.Sigmoid)
-            sig[e] = sg
+        def by_half(bank):
+            return bank[:].rearrange("p (q u t) -> p u q t", u=2, t=2)
 
-        def mul(e):
-            h = keep.tile([P, H], BF16, name=f"h{e}")
-            nc.vector.tensor_tensor(h[:], acc["b", e][:], sig[e][:], MULT)
-            hid[e] = h
+        def front(g):
+            pair = (2 * g, 2 * g + 1)
+            a = [first(e, 0, s1_sb) for e in pair]
+            b = [first(e, 1, s3_sb) for e in pair]
+            for c, e in enumerate(pair):
+                sg = keep.tile([P, 2, P, 2], F32, name=f"sg{e}")
+                nc.scalar.activation(sg[:], by_half(a[c]), ACT.Sigmoid)
+                h = keep.tile([P, 2, P, 2], BF16, name=f"h{e}")
+                nc.vector.tensor_tensor(h[:], by_half(b[c]), sg[:], MULT)
+                hid[e] = h
 
-        def turn(g):
-            tp = psum.tile([P, 2, 2, C], F32, name="tp")
+        def middle(g):
+            tp = psum.tile([P, 2, 2, C], F32, name="bank")
             for c in range(2):
-                words = hid[2 * g + c][:].bitcast(F32)
+                words = hid[2 * g + c][:].rearrange("p u q t -> p (u q t)").bitcast(F32)
                 for u in range(2):
-                    nc.tensor.transpose(tp[:, c, u, :], words[:, u::2], ident[:])
-            turned[g] = tp
-
-        def evt(g):
+                    nc.tensor.transpose(tp[:, c, u, :], words[:, P * u : P * (u + 1)], ident[:])
             h4 = work.tile([P, 2, C, 4], BF16, name="h4", align_bytes=64)
             h4w = h4[:].rearrange("p e c t -> p (e c t)")
             nc.scalar.copy(
                 h4w.bitcast(F32).rearrange("p (e c u) -> p e c u", e=2, u=2),
-                turned[g][:].rearrange("p e u c -> p e c u"),
+                tp[:].rearrange("p e u c -> p e c u"),
             )
-            h4s[g] = h4w
-
-        def hquant(g):
             hq = work.tile([P, GS], U32, name="hq", align_bytes=64)
             hsc = work.tile([P, GS], U8, name="hsc", align_bytes=64)
-            nc.vector.quantize_mx(out=hq[:].bitcast(FP8X4), scales=hsc[:], in_=h4s[g])
+            nc.vector.quantize_mx(out=hq[:].bitcast(FP8X4), scales=hsc[:], in_=h4w)
             hqs[g] = (hq, hsc)
 
         def second(g):
             hq, hsc = hqs[g]
-            y = psum.tile([P, 2, GS], F32, name="y")
-            for c in range(2):
-                cols = slice(C * c, C * (c + 1))
-                for n in range(2):
+            y = psum.tile([P, 2, GS], F32, name="bank")
+            for n in range(2):
+                for c in range(2):
+                    cols = slice(C * c, C * (c + 1))
                     nc.tensor.matmul_mx(
                         out=y[:, n, cols],
                         lhsT=w2_sb[:, 2 * g + c, 2 * P * n : 2 * P * (n + 1)].bitcast(FP4X4),
@@ -179,80 +152,63 @@ def tile_moe_two_glu_sigmoid_kernel(
                     )
             ys[g] = y
 
-        def evy(g):
-            y_sb = work.tile([P, 2, GS], F32, name="y_sb")
-            nc.scalar.copy(y_sb[:], ys[g][:])
-            ysb[g] = y_sb
-
-        def scatter(g, n):
+        def back(g, n):
+            y_sb = keep.tile([P, GS], F32, name=f"h{2 * g if n == 0 else E - 1 - 2 * g}")
+            nc.scalar.copy(y_sb[:], ys[g][:, n, :])
             nc.vector.tensor_tensor(
-                wins[n][:].indirect(dst_sb[:, GO * g : GO * (g + 1)]),
-                ysb[g][:, n, :],
-                gate_sb[:, n, GS * g : GS * (g + 1)],
-                MULT,
+                wins[n][:].indirect(slots(dst_sb, g)), y_sb[:], gate_sb[:, GS * g : GS * (g + 1)], MULT
             )
             if g == G - 1:
                 nc.sync.dma_start(out[P * n : P * (n + 1), :], wins[n][:])
 
         nc.vector.tensor_copy(p01[:, 0, :], planes[0][:].indirect(offs_sb[:]))
-        nc.vector.tensor_copy(p01[:, 1, :], planes[1][:].indirect(offs_sb[:]))
-        precast(0)
-        precast(1)
-        precast(2)
-        gather(2, 0)
-        gather(2, 1)
-        gather(3, 0)
-        cast(0, "S")
-        gather(3, 1)
-        cast(1, "S")
-        gather(3, 2)
-        quant(0)
-        gather(2, 2)
-        quant(1)
-        first(0, "a", w1_sb, s1_sb)
-        first(1, "a", w1_sb, s1_sb)
-        first(0, "b", w3_sb, s3_sb)
-        first(1, "b", w3_sb, s3_sb)
-        sigm(0)
-        sigm(1)
-        mul(0)
-        mul(1)
-        first(2, "a", w1_sb, s1_sb)
-        sigm(2)
-        cast(2, "S")
-        quant(2)
-        first(3, "a", w1_sb, s1_sb)
-        first(2, "b", w3_sb, s3_sb)
-        first(3, "b", w3_sb, s3_sb)
-        sigm(3)
-        mul(2)
-        mul(3)
-        turn(0)
-        evt(0)
-        hquant(0)
-        first(4, "a", w1_sb, s1_sb)
-        first(5, "a", w1_sb, s1_sb)
-        first(4, "b", w3_sb, s3_sb)
-        first(5, "b", w3_sb, s3_sb)
-        sigm(4)
-        sigm(5)
-        mul(4)
-        mul(5)
-        second(0)
-        evy(0)
-        turn(1)
-        evt(1)
-        turn(2)
-        evt(2)
-        scatter(0, 0)
-        hquant(1)
-        hquant(2)
-        second(1)
-        second(2)
-        evy(1)
-        evy(2)
-        scatter(0, 1)
-        scatter(1, 0)
-        scatter(2, 0)
-        scatter(1, 1)
-        scatter(2, 1)
+        for g in range(G):
+            nc.vector.tensor_copy(p01[:, 1, GS * g : GS * (g + 1)], planes[1][:].indirect(slots(offs_sb, g)))
+            nc.scalar.copy(x4[g][:, :, 0:2], p01[:, :, GS * g : GS * (g + 1)].rearrange("p t c -> p c t"))
+        for j in (2, 3):
+            for g in range(G):
+                nc.vector.tensor_copy(p23[g][:, j - 2, :], planes[j][:].indirect(slots(offs_sb, g)))
+        for g in range(G):
+            cast = nc.vector.tensor_copy if g == G - 1 else nc.scalar.copy
+            cast(x4[g][:, :, 2:4], p23[g][:].rearrange("p t c -> p c t"))
+            quant(g)
+
+        w1_first = keep.tile([P, 2, 2 * H], U8, name="w1_first", align_bytes=64)
+        w3_first = keep.tile([P, 2, 2 * H], U8, name="plane0", align_bytes=64)
+        w13 = [(w1_first[:], w3_first[:])]
+        for g in range(1, G):
+            both = keep.tile([P, 2, 2, 2 * H], U8, name=f"plane{g}", align_bytes=64)
+            w13.append((both[:, 0, :, :], both[:, 1, :, :]))
+        w2_sb = keep.tile([P, E, 2 * N], U8, name="plane3", align_bytes=64)
+        gate_sb = keep.tile([P, E * C], F32, name="p01")
+        for g in range(G):
+            for m, (words, plane, scales) in enumerate(((w1_words, s1_sb, w1_scales), (w3_words, s3_sb, w3_scales))):
+                if g == 0:
+                    load_scales(plane, scales)
+                load_words(w13[g][m], words, 2 * g, 2 * g + 2)
+        load_scales(s2_sb, w2_scales)
+        load_words(w2_sb[:], w2_words, 0, E)
+        nc.sync.dma_start(out=gate_sb[:], in_=gate[0:P, :])
+
+        idle = psum.tile([P, H], F32, name="bank")
+        for i in range(3):
+            nc.tensor.matmul_mx(
+                out=idle[:],
+                lhsT=w1_first[:, 0, 0 : 2 * P].bitcast(FP4X4),
+                lhsT_scale=zs[:, 0:P],
+                rhs=zq[:].bitcast(FP8X4),
+                rhs_scale=zs[:],
+                start=True,
+                stop=True,
+            )
+
+        for s in range(G + 3):
+            if s < G:
+                front(s)
+            if 1 <= s <= G:
+                middle(s - 1)
+            if s >= 3:
+                back(s - 3, 1)
+            if 2 <= s < G + 2:
+                second(s - 2)
+                back(s - 2, 0)

@@ -34,6 +34,7 @@ def tile_moe_two_glu_sigmoid_kernel(
 
         offs_sb = keep.tile([P, E * C // 16], U16, name="offs_sb")
         dst_sb = keep.tile([P, E * C // 16], U16, name="dst_sb")
+        zero = keep.tile([P, 1], F32, name="zero")
         warm = keep.tile([P, 1], F32, name="warm")
         ident = keep.tile([P, P], F32, name="ident")
         planes = [keep.tile([P, T], F32, name=f"plane{j}", align_bytes=64) for j in range(4)]
@@ -41,6 +42,7 @@ def tile_moe_two_glu_sigmoid_kernel(
         s3_sb = keep.tile([P, E, H], U8, name="s3_sb", align_bytes=64)
         s2_sb = keep.tile([P, E, N], U8, name="s2_sb", align_bytes=64)
         wins = [keep.tile([P, T], F32, name=f"win{h}", align_bytes=64) for h in range(2)]
+        zb = keep.tile([P, 4 * H], BF16, name="zb", align_bytes=64)
         zq = keep.tile([P, H], U32, name="zq", align_bytes=64)
         zs = keep.tile([P, H], U8, name="zs", align_bytes=64)
         p01 = keep.tile([P, 2, E * C], F32, name="p01")
@@ -55,14 +57,15 @@ def tile_moe_two_glu_sigmoid_kernel(
         for j in range(4):
             nc.sync.dma_start(out=planes[j][:], in_=xv[:, j, :])
 
-        nc.vector.memset(warm[:], 0.0)
-        nc.scalar.activation(warm[:], warm[:], ACT.Sigmoid)
+        nc.vector.memset(zero[:], 0.0)
+        nc.scalar.activation(warm[:], zero[:], ACT.Sigmoid)
         for t in (s1_sb, s3_sb, s2_sb):
             nc.vector.memset(t[:].rearrange("p e i -> p (e i)").bitcast(I32), 0)
         for w in wins:
-            nc.gpsimd.memset(w[:], 0.0)
+            nc.scalar.copy(w[:], zero[:].to_broadcast([P, T]))
         make_identity(nc, ident[:])
-        nc.vector.quantize_mx(out=zq[:].bitcast(FP8X4), scales=zs[:], in_=wins[0][:].bitcast(BF16)[:, 0 : 4 * H])
+        nc.gpsimd.memset(zb[:].bitcast(I32), 0)
+        nc.vector.quantize_mx(out=zq[:].bitcast(FP8X4), scales=zs[:], in_=zb[:])
 
         def load_scales(tile, dram):
             flat = tile[:].rearrange("p e i -> p (e i)").bitcast(I32)
@@ -169,8 +172,7 @@ def tile_moe_two_glu_sigmoid_kernel(
             for g in range(G):
                 nc.vector.tensor_copy(p23[g][:, j - 2, :], planes[j][:].indirect(slots(offs_sb, g)))
         for g in range(G):
-            cast = nc.vector.tensor_copy if g == G - 1 else nc.scalar.copy
-            cast(x4[g][:, :, 2:4], p23[g][:].rearrange("p t c -> p c t"))
+            nc.scalar.copy(x4[g][:, :, 2:4], p23[g][:].rearrange("p t c -> p c t"))
             quant(g)
 
         w1_first = keep.tile([P, 2, 2 * H], U8, name="w1_first", align_bytes=64)

@@ -51,11 +51,12 @@ def tile_moe_two_glu_sigmoid_kernel(
         xq = [keep.tile([P, GS], U32, name=f"xq_{g}", align_bytes=64) for g in range(G)]
         xs = [keep.tile([P, GS], U8, name=f"xs_{g}", align_bytes=64) for g in range(G)]
 
-        nc.sync.dma_start(offs_sb[:], offs)
-        nc.sync.dma_start(dst_sb[:], dst)
         xv = xT.rearrange("(p j) t -> p j t", j=4)
         for j in range(4):
             nc.sync.dma_start(out=planes[j][:], in_=xv[:, j, :])
+            if j == 0:
+                nc.sync.dma_start(offs_sb[:], offs)
+                nc.sync.dma_start(dst_sb[:], dst)
 
         nc.vector.memset(zero[:], 0.0)
         nc.scalar.activation(warm[:], zero[:], ACT.Sigmoid)
@@ -175,7 +176,7 @@ def tile_moe_two_glu_sigmoid_kernel(
             nc.scalar.copy(x4[g][:, :, 2:4], p23[g][:].rearrange("p t c -> p c t"))
             quant(g)
 
-        w1_first = keep.tile([P, 2, 2 * H], U8, name="w1_first", align_bytes=64)
+        w1_first = keep.tile([P, 2, 2 * H], U8, name="zb", align_bytes=64)
         w3_first = keep.tile([P, 2, 2 * H], U8, name="plane0", align_bytes=64)
         w13 = [(w1_first[:], w3_first[:])]
         for g in range(1, G):
@@ -183,17 +184,18 @@ def tile_moe_two_glu_sigmoid_kernel(
             w13.append((both[:, 0, :, :], both[:, 1, :, :]))
         w2_sb = keep.tile([P, E, 2 * N], U8, name="plane3", align_bytes=64)
         gate_sb = keep.tile([P, E * C], F32, name="p01")
+        load_scales(s1_sb, w1_scales)
         for g in range(G):
-            for m, (words, plane, scales) in enumerate(((w1_words, s1_sb, w1_scales), (w3_words, s3_sb, w3_scales))):
-                if g == 0:
-                    load_scales(plane, scales)
-                load_words(w13[g][m], words, 2 * g, 2 * g + 2)
+            load_words(w13[g][0], w1_words, 2 * g, 2 * g + 2)
+            load_words(w13[g][1], w3_words, 2 * g, 2 * g + 2)
+            if g == 0:
+                load_scales(s3_sb, w3_scales)
         load_scales(s2_sb, w2_scales)
         load_words(w2_sb[:], w2_words, 0, E)
         nc.sync.dma_start(out=gate_sb[:], in_=gate[0:P, :])
 
         idle = psum.tile([P, H], F32, name="bank")
-        for i in range(3):
+        for i in range(2):
             nc.tensor.matmul_mx(
                 out=idle[:],
                 lhsT=w1_first[:, 0, 0 : 2 * P].bitcast(FP4X4),

@@ -45,9 +45,12 @@ def tile_moe_two_glu_sigmoid_kernel(
         zb = keep.tile([P, 4 * H], BF16, name="zb", align_bytes=64)
         zq = keep.tile([P, H], U32, name="zq", align_bytes=64)
         zs = keep.tile([P, H], U8, name="zs", align_bytes=64)
-        p01 = keep.tile([P, 2, E * C], F32, name="p01")
-        p23 = [keep.tile([P, 2, GS], F32, name=f"p23_{g}") for g in range(G)]
-        x4 = [keep.tile([P, GS, 4], BF16, name=f"x4_{g}", align_bytes=64) for g in range(G)]
+        p01 = keep.tile([P, 2, (G - 1) * GS], F32, name="p01")
+        five = keep.tile([P, 5, GS], F32, name="five")
+        rows = five[:, 1:5, :]
+        p23_1 = keep.tile([P, 2, GS], F32, name="p23_1")
+        p23 = [five[:, 0:4:3, :], p23_1[:]]
+        x4 = [keep.tile([P, GS, 4], BF16, name=f"x4_{g}", align_bytes=64) for g in range(G - 1)]
         xq = [keep.tile([P, GS], U32, name=f"xq_{g}", align_bytes=64) for g in range(G)]
         xs = [keep.tile([P, GS], U8, name=f"xs_{g}", align_bytes=64) for g in range(G)]
 
@@ -86,9 +89,11 @@ def tile_moe_two_glu_sigmoid_kernel(
         def slots(lst, g):
             return lst[:, GO * g : GO * (g + 1)]
 
-        def quant(g):
+        def quant(g, cols):
             nc.vector.quantize_mx(
-                out=xq[g][:].bitcast(FP8X4), scales=xs[g][:], in_=x4[g][:].rearrange("p c t -> p (c t)")
+                out=xq[g][:, cols].bitcast(FP8X4),
+                scales=xs[g][:, cols],
+                in_=x4[g][:, cols, :].rearrange("p c t -> p (c t)"),
             )
 
         hid, hqs, ys = {}, {}, {}
@@ -123,17 +128,17 @@ def tile_moe_two_glu_sigmoid_kernel(
                 hid[e] = h
 
         def middle(g):
-            tp = psum.tile([P, 2, 2, C], F32, name="bank")
-            for c in range(2):
-                words = hid[2 * g + c][:].rearrange("p u q t -> p (u q t)").bitcast(F32)
-                for u in range(2):
-                    nc.tensor.transpose(tp[:, c, u, :], words[:, P * u : P * (u + 1)], ident[:])
             h4 = work.tile([P, 2, C, 4], BF16, name="h4", align_bytes=64)
             h4w = h4[:].rearrange("p e c t -> p (e c t)")
-            nc.scalar.copy(
-                h4w.bitcast(F32).rearrange("p (e c u) -> p e c u", e=2, u=2),
-                tp[:].rearrange("p e u c -> p e c u"),
-            )
+            for c in range(2):
+                tp = psum.tile([P, 2, C], F32, name="bank")
+                words = hid[2 * g + c][:].rearrange("p u q t -> p (u q t)").bitcast(F32)
+                for u in range(2):
+                    nc.tensor.transpose(tp[:, u, :], words[:, P * u : P * (u + 1)], ident[:])
+                nc.scalar.copy(
+                    h4w.bitcast(F32)[:, 2 * C * c : 2 * C * (c + 1)].rearrange("p (c u) -> p c u", u=2),
+                    tp[:].rearrange("p u c -> p c u"),
+                )
             hq = work.tile([P, GS], U32, name="hq", align_bytes=64)
             hsc = work.tile([P, GS], U8, name="hsc", align_bytes=64)
             nc.vector.quantize_mx(out=hq[:].bitcast(FP8X4), scales=hsc[:], in_=h4w)
@@ -141,12 +146,13 @@ def tile_moe_two_glu_sigmoid_kernel(
 
         def second(g):
             hq, hsc = hqs[g]
-            y = psum.tile([P, 2, GS], F32, name="bank")
             for n in range(2):
+                y = psum.tile([P, GS], F32, name="bank")
+                ys[g, n] = y
                 for c in range(2):
                     cols = slice(C * c, C * (c + 1))
                     nc.tensor.matmul_mx(
-                        out=y[:, n, cols],
+                        out=y[:, cols],
                         lhsT=w2_sb[:, 2 * g + c, 2 * P * n : 2 * P * (n + 1)].bitcast(FP4X4),
                         lhsT_scale=s2_sb[:, 2 * g + c, P * n : P * (n + 1)],
                         rhs=hq[:, cols].bitcast(FP8X4),
@@ -154,35 +160,50 @@ def tile_moe_two_glu_sigmoid_kernel(
                         start=True,
                         stop=True,
                     )
-            ys[g] = y
 
         def back(g, n):
             y_sb = keep.tile([P, GS], F32, name=f"h{2 * g if n == 0 else E - 1 - 2 * g}")
-            nc.scalar.copy(y_sb[:], ys[g][:, n, :])
+            nc.scalar.copy(y_sb[:], ys[g, n][:])
             nc.vector.tensor_tensor(
                 wins[n][:].indirect(slots(dst_sb, g)), y_sb[:], gate_sb[:, GS * g : GS * (g + 1)], MULT
             )
             if g == G - 1:
                 nc.sync.dma_start(out[P * n : P * (n + 1), :], wins[n][:])
 
-        nc.vector.tensor_copy(p01[:, 0, :], planes[0][:].indirect(offs_sb[:]))
-        for g in range(G):
-            nc.vector.tensor_copy(p01[:, 1, GS * g : GS * (g + 1)], planes[1][:].indirect(slots(offs_sb, g)))
-            nc.scalar.copy(x4[g][:, :, 0:2], p01[:, :, GS * g : GS * (g + 1)].rearrange("p t c -> p c t"))
-        for j in (2, 3):
-            for g in range(G):
-                nc.vector.tensor_copy(p23[g][:, j - 2, :], planes[j][:].indirect(slots(offs_sb, g)))
-        for g in range(G):
-            nc.scalar.copy(x4[g][:, :, 2:4], p23[g][:].rearrange("p t c -> p c t"))
-            quant(g)
+        def pick(target, j, g0, g1):
+            nc.vector.tensor_copy(target, planes[j][:].indirect(offs_sb[:, GO * g0 : GO * g1]))
 
-        w1_first = keep.tile([P, 2, 2 * H], U8, name="zb", align_bytes=64)
+        last = G - 1
+        pick(p01[:, 0, :], 0, 0, last)
+        pick(rows[:, 0, :], 0, last, G)
+        for g in range(last):
+            pick(p01[:, 1, GS * g : GS * (g + 1)], 1, g, g + 1)
+            nc.scalar.copy(x4[g][:, :, 0:2], p01[:, :, GS * g : GS * (g + 1)].rearrange("p t c -> p c t"))
+        pick(rows[:, 1, :], 1, last, G)
+        for j in (2, 3):
+            for g in range(last):
+                pick(p23[g][:, j - 2, :], j, g, g + 1)
+        pick(rows[:, 3, :], 3, last, G)
+        for c in range(2):
+            cols = slice(C * c, C * (c + 1))
+            nc.scalar.copy(x4[0][:, cols, 2:4], p23[0][:, :, cols].rearrange("p t c -> p c t"))
+            quant(0, cols)
+        pick(rows[:, 2, :], 2, last, G)
+        nc.scalar.copy(x4[1][:, :, 2:4], p23[1].rearrange("p t c -> p c t"))
+        x4.append(keep.tile([P, GS, 4], BF16, name="x4_0", align_bytes=64))
+        nc.vector.tensor_copy(
+            x4[last][:].rearrange("p (c i) t -> p c t i", i=4), rows.rearrange("p t (c i) -> p c t i", i=4)
+        )
+        for g in range(1, G):
+            quant(g, slice(0, GS))
+
+        w1_first = keep.tile([P, 2, 2 * H], U8, name="w1_first", align_bytes=64)
         w3_first = keep.tile([P, 2, 2 * H], U8, name="plane0", align_bytes=64)
         w13 = [(w1_first[:], w3_first[:])]
         for g in range(1, G):
-            both = keep.tile([P, 2, 2, 2 * H], U8, name=f"plane{g}", align_bytes=64)
+            both = keep.tile([P, 2, 2, 2 * H], U8, name=("plane1", "plane3")[g - 1], align_bytes=64)
             w13.append((both[:, 0, :, :], both[:, 1, :, :]))
-        w2_sb = keep.tile([P, E, 2 * N], U8, name="plane3", align_bytes=64)
+        w2_sb = keep.tile([P, E, 2 * N], U8, name="plane2", align_bytes=64)
         gate_sb = keep.tile([P, E * C], F32, name="p01")
         load_scales(s1_sb, w1_scales)
         for g in range(G):

@@ -18,9 +18,11 @@ ACT = mybir.ActivationFunctionType
 MULT = mybir.AluOpType.mult
 
 P = 128
-G = 3
+G = E // 2
+LAST = G - 1
 GS = 2 * C
 GO = GS // 16
+WARM_PASSES = 2
 
 
 def tile_moe_two_glu_sigmoid_kernel(
@@ -29,7 +31,7 @@ def tile_moe_two_glu_sigmoid_kernel(
     nc = tc.nc
     with ExitStack() as ctx:
         keep = ctx.enter_context(tc.tile_pool(name="keep", bufs=1))
-        work = ctx.enter_context(tc.tile_pool(name="work", bufs=3))
+        work = ctx.enter_context(tc.tile_pool(name="work", bufs=G))
         psum = ctx.enter_context(tc.psum_pool(name="psum", bufs=8))
 
         offs_sb = keep.tile([P, E * C // 16], U16, name="offs_sb")
@@ -37,46 +39,46 @@ def tile_moe_two_glu_sigmoid_kernel(
         zero = keep.tile([P, 1], F32, name="zero")
         warm = keep.tile([P, 1], F32, name="warm")
         ident = keep.tile([P, P], F32, name="ident")
-        planes = [keep.tile([P, T], F32, name=f"plane{j}", align_bytes=64) for j in range(4)]
+        planes = [keep.tile([P, T], F32, name=f"plane{t}", align_bytes=64) for t in range(4)]
         s1_sb = keep.tile([P, E, H], U8, name="s1_sb", align_bytes=64)
         s3_sb = keep.tile([P, E, H], U8, name="s3_sb", align_bytes=64)
         s2_sb = keep.tile([P, E, N], U8, name="s2_sb", align_bytes=64)
-        wins = [keep.tile([P, T], F32, name=f"win{h}", align_bytes=64) for h in range(2)]
-        zb = keep.tile([P, 4 * H], BF16, name="zb", align_bytes=64)
-        zq = keep.tile([P, H], U32, name="zq", align_bytes=64)
-        zs = keep.tile([P, H], U8, name="zs", align_bytes=64)
-        p01 = keep.tile([P, 2, (G - 1) * GS], F32, name="p01")
+        wins = [keep.tile([P, T], F32, name=f"win{n}", align_bytes=64) for n in range(2)]
+        zero_in = keep.tile([P, 4 * H], BF16, name="zero_in", align_bytes=64)
+        zero_codes = keep.tile([P, H], U32, name="zero_codes", align_bytes=64)
+        zero_scales = keep.tile([P, H], U8, name="zero_scales", align_bytes=64)
+        p01 = keep.tile([P, 2, LAST * GS], F32, name="p01")
         five = keep.tile([P, 5, GS], F32, name="five")
-        rows = five[:, 1:5, :]
+        last_rows = five[:, 1:5, :]
         p23_1 = keep.tile([P, 2, GS], F32, name="p23_1")
         p23 = [five[:, 0:4:3, :], p23_1[:]]
-        x4 = [keep.tile([P, GS, 4], BF16, name=f"x4_{g}", align_bytes=64) for g in range(G - 1)]
+        x4 = [keep.tile([P, GS, 4], BF16, name=f"x4_{g}", align_bytes=64) for g in range(LAST)]
         xq = [keep.tile([P, GS], U32, name=f"xq_{g}", align_bytes=64) for g in range(G)]
         xs = [keep.tile([P, GS], U8, name=f"xs_{g}", align_bytes=64) for g in range(G)]
 
-        xv = xT.rearrange("(p j) t -> p j t", j=4)
-        for j in range(4):
-            nc.sync.dma_start(out=planes[j][:], in_=xv[:, j, :])
-            if j == 0:
+        x_rows = xT.rearrange("(p t) j -> p t j", t=4)
+        for t in range(4):
+            nc.sync.dma_start(out=planes[t][:], in_=x_rows[:, t, :])
+            if t == 0:
                 nc.sync.dma_start(offs_sb[:], offs)
                 nc.sync.dma_start(dst_sb[:], dst)
 
         nc.vector.memset(zero[:], 0.0)
         nc.scalar.activation(warm[:], zero[:], ACT.Sigmoid)
-        for t in (s1_sb, s3_sb, s2_sb):
-            nc.vector.memset(t[:].rearrange("p e i -> p (e i)").bitcast(I32), 0)
-        for w in wins:
-            nc.scalar.copy(w[:], zero[:].to_broadcast([P, T]))
+        for scales_sb in (s1_sb, s3_sb, s2_sb):
+            nc.vector.memset(scales_sb[:].rearrange("p e i -> p (e i)").bitcast(I32), 0)
+        nc.scalar.copy(zero_in[:].bitcast(F32), zero[:].to_broadcast([P, 2 * H]))
+        nc.vector.quantize_mx(out=zero_codes[:].bitcast(FP8X4), scales=zero_scales[:], in_=zero_in[:])
+        for win in wins:
+            nc.scalar.copy(win[:], zero[:].to_broadcast([P, T]))
         make_identity(nc, ident[:])
-        nc.gpsimd.memset(zb[:].bitcast(I32), 0)
-        nc.vector.quantize_mx(out=zq[:].bitcast(FP8X4), scales=zs[:], in_=zb[:])
 
-        def load_scales(tile, dram):
-            flat = tile[:].rearrange("p e i -> p (e i)").bitcast(I32)
-            w = tile.shape[2] // 4
+        def load_scales(scales_sb, dram):
+            flat = scales_sb[:].rearrange("p e i -> p (e i)").bitcast(I32)
+            width = scales_sb.shape[2] // 4
             for r in range(4):
                 nc.sync.dma_start(
-                    out=flat[r:P:32, :].rearrange("q (e i) -> q e i", i=w),
+                    out=flat[r:P:32, :].rearrange("q (e i) -> q e i", i=width),
                     in_=dram[:, 0, r:16:4, :].rearrange("e q i -> q e i").bitcast(I32),
                 )
 
@@ -86,40 +88,94 @@ def tile_moe_two_glu_sigmoid_kernel(
                 in_=dram[e0:e1, 0, :, :].rearrange("e p b -> p e b").bitcast(I32),
             )
 
-        def slots(lst, g):
-            return lst[:, GO * g : GO * (g + 1)]
+        def gather(target, t, g0, g1):
+            nc.vector.tensor_copy(target, planes[t][:].indirect(offs_sb[:, GO * g0 : GO * g1]))
 
-        def quant(g, cols):
+        def quantise_x(g, cols):
             nc.vector.quantize_mx(
                 out=xq[g][:, cols].bitcast(FP8X4),
                 scales=xs[g][:, cols],
                 in_=x4[g][:, cols, :].rearrange("p c t -> p (c t)"),
             )
 
-        hid, hqs, ys = {}, {}, {}
-
-        def first(e, m, s):
-            g, c = divmod(e, 2)
+        gather(p01[:, 0, :], 0, 0, LAST)
+        gather(last_rows[:, 0, :], 0, LAST, G)
+        for g in range(LAST):
+            gather(p01[:, 1, GS * g : GS * (g + 1)], 1, g, g + 1)
+            nc.scalar.copy(x4[g][:, :, 0:2], p01[:, :, GS * g : GS * (g + 1)].rearrange("p t c -> p c t"))
+        gather(last_rows[:, 1, :], 1, LAST, G)
+        for t in (2, 3):
+            for g in range(LAST):
+                gather(p23[g][:, t - 2, :], t, g, g + 1)
+        gather(last_rows[:, 3, :], 3, LAST, G)
+        for c in range(2):
             cols = slice(C * c, C * (c + 1))
-            t = psum.tile([P, H], F32, name="bank")
+            nc.scalar.copy(x4[0][:, cols, 2:4], p23[0][:, :, cols].rearrange("p t c -> p c t"))
+            quantise_x(0, cols)
+        gather(last_rows[:, 2, :], 2, LAST, G)
+        nc.scalar.copy(x4[1][:, :, 2:4], p23[1].rearrange("p t c -> p c t"))
+        x4.append(keep.tile([P, GS, 4], BF16, name="x4_last", tag="x4_0", align_bytes=64))
+        nc.vector.tensor_copy(
+            x4[LAST][:].rearrange("p (c i) t -> p c t i", i=4), last_rows.rearrange("p t (c i) -> p c t i", i=4)
+        )
+        for g in range(1, G):
+            quantise_x(g, slice(0, GS))
+
+        w1_first = keep.tile([P, 2, 2 * H], U8, name="w1_first", align_bytes=64)
+        w3_first = keep.tile([P, 2, 2 * H], U8, name="w3_first", tag="plane0", align_bytes=64)
+        w13_1 = keep.tile([P, 2, 2, 2 * H], U8, name="w13_1", tag="plane1", align_bytes=64)
+        w13_2 = keep.tile([P, 2, 2, 2 * H], U8, name="w13_2", tag="plane3", align_bytes=64)
+        w1_sb = [w1_first[:], w13_1[:, 0, :, :], w13_2[:, 0, :, :]]
+        w3_sb = [w3_first[:], w13_1[:, 1, :, :], w13_2[:, 1, :, :]]
+        w2_sb = keep.tile([P, E, 2 * N], U8, name="w2_sb", tag="plane2", align_bytes=64)
+        gate_sb = keep.tile([P, E * C], F32, name="gate_sb", tag="p01")
+        load_scales(s1_sb, w1_scales)
+        for g in range(G):
+            load_words(w1_sb[g], w1_words, 2 * g, 2 * g + 2)
+            load_words(w3_sb[g], w3_words, 2 * g, 2 * g + 2)
+            if g == 0:
+                load_scales(s3_sb, w3_scales)
+        load_scales(s2_sb, w2_scales)
+        for e0, e1 in ((0, 2), (2, E)):
+            load_words(w2_sb[:, e0:e1, :], w2_words, e0, e1)
+            nc.sync.dma_start(out=gate_sb[:, C * e0 : C * e1], in_=gate[0:P, C * e0 : C * e1])
+
+        unread = psum.tile([P, H], F32, name="bank")
+        for i in range(WARM_PASSES):
             nc.tensor.matmul_mx(
-                out=t[:],
-                lhsT=xq[g][:, cols].bitcast(FP8X4),
-                lhsT_scale=xs[g][:, cols],
-                rhs=w13[g][m][:, c, :].bitcast(FP4X4),
-                rhs_scale=s[:, e, :],
+                out=unread[:],
+                lhsT=w1_first[:, 0, 0 : 2 * P].bitcast(FP4X4),
+                lhsT_scale=zero_scales[:, 0:P],
+                rhs=zero_codes[:].bitcast(FP8X4),
+                rhs_scale=zero_scales[:],
                 start=True,
                 stop=True,
             )
-            return t
 
-        def by_half(bank):
-            return bank[:].rearrange("p (q u t) -> p u q t", u=2, t=2)
+        hid, h_codes, y_banks = {}, {}, {}
 
-        def front(g):
+        def first_product(e, words, scales_sb):
+            g, c = divmod(e, 2)
+            cols = slice(C * c, C * (c + 1))
+            sums = psum.tile([P, H], F32, name="bank")
+            nc.tensor.matmul_mx(
+                out=sums[:],
+                lhsT=xq[g][:, cols].bitcast(FP8X4),
+                lhsT_scale=xs[g][:, cols],
+                rhs=words[g][:, c, :].bitcast(FP4X4),
+                rhs_scale=scales_sb[:, e, :],
+                start=True,
+                stop=True,
+            )
+            return sums
+
+        def by_half(sums):
+            return sums[:].rearrange("p (q u d) -> p u q d", u=2, d=2)
+
+        def hidden(g):
             pair = (2 * g, 2 * g + 1)
-            a = [first(e, 0, s1_sb) for e in pair]
-            b = [first(e, 1, s3_sb) for e in pair]
+            a = [first_product(e, w1_sb, s1_sb) for e in pair]
+            b = [first_product(e, w3_sb, s3_sb) for e in pair]
             for c, e in enumerate(pair):
                 sg = keep.tile([P, 2, P, 2], F32, name=f"sg{e}")
                 nc.scalar.activation(sg[:], by_half(a[c]), ACT.Sigmoid)
@@ -127,28 +183,28 @@ def tile_moe_two_glu_sigmoid_kernel(
                 nc.vector.tensor_tensor(h[:], by_half(b[c]), sg[:], MULT)
                 hid[e] = h
 
-        def middle(g):
+        def turn_and_quantise(g):
             h4 = work.tile([P, 2, C, 4], BF16, name="h4", align_bytes=64)
-            h4w = h4[:].rearrange("p e c t -> p (e c t)")
+            h4_flat = h4[:].rearrange("p e c t -> p (e c t)")
             for c in range(2):
-                tp = psum.tile([P, 2, C], F32, name="bank")
-                words = hid[2 * g + c][:].rearrange("p u q t -> p (u q t)").bitcast(F32)
+                turned = psum.tile([P, 2, C], F32, name="bank")
+                pairs = hid[2 * g + c][:].rearrange("p u q d -> p (u q d)").bitcast(F32)
                 for u in range(2):
-                    nc.tensor.transpose(tp[:, u, :], words[:, P * u : P * (u + 1)], ident[:])
+                    nc.tensor.transpose(turned[:, u, :], pairs[:, P * u : P * (u + 1)], ident[:])
                 nc.scalar.copy(
-                    h4w.bitcast(F32)[:, 2 * C * c : 2 * C * (c + 1)].rearrange("p (c u) -> p c u", u=2),
-                    tp[:].rearrange("p u c -> p c u"),
+                    h4_flat.bitcast(F32)[:, 2 * C * c : 2 * C * (c + 1)].rearrange("p (c u) -> p c u", u=2),
+                    turned[:].rearrange("p u c -> p c u"),
                 )
             hq = work.tile([P, GS], U32, name="hq", align_bytes=64)
-            hsc = work.tile([P, GS], U8, name="hsc", align_bytes=64)
-            nc.vector.quantize_mx(out=hq[:].bitcast(FP8X4), scales=hsc[:], in_=h4w)
-            hqs[g] = (hq, hsc)
+            hs = work.tile([P, GS], U8, name="hs", align_bytes=64)
+            nc.vector.quantize_mx(out=hq[:].bitcast(FP8X4), scales=hs[:], in_=h4_flat)
+            h_codes[g] = (hq, hs)
 
-        def second(g):
-            hq, hsc = hqs[g]
+        def second_product(g):
+            hq, hs = h_codes[g]
             for n in range(2):
                 y = psum.tile([P, GS], F32, name="bank")
-                ys[g, n] = y
+                y_banks[g, n] = y
                 for c in range(2):
                     cols = slice(C * c, C * (c + 1))
                     nc.tensor.matmul_mx(
@@ -156,84 +212,31 @@ def tile_moe_two_glu_sigmoid_kernel(
                         lhsT=w2_sb[:, 2 * g + c, 2 * P * n : 2 * P * (n + 1)].bitcast(FP4X4),
                         lhsT_scale=s2_sb[:, 2 * g + c, P * n : P * (n + 1)],
                         rhs=hq[:, cols].bitcast(FP8X4),
-                        rhs_scale=hsc[:, cols],
+                        rhs_scale=hs[:, cols],
                         start=True,
                         stop=True,
                     )
 
-        def back(g, n):
-            y_sb = keep.tile([P, GS], F32, name=f"h{2 * g if n == 0 else E - 1 - 2 * g}")
-            nc.scalar.copy(y_sb[:], ys[g, n][:])
+        def scatter(g, n):
+            host = 2 * g if n == 0 else E - 1 - 2 * g
+            y_sb = keep.tile([P, GS], F32, name=f"y{g}{n}", tag=f"h{host}")
+            nc.scalar.copy(y_sb[:], y_banks[g, n][:])
             nc.vector.tensor_tensor(
-                wins[n][:].indirect(slots(dst_sb, g)), y_sb[:], gate_sb[:, GS * g : GS * (g + 1)], MULT
+                wins[n][:].indirect(dst_sb[:, GO * g : GO * (g + 1)]),
+                y_sb[:],
+                gate_sb[:, GS * g : GS * (g + 1)],
+                MULT,
             )
-            if g == G - 1:
+            if g == LAST:
                 nc.sync.dma_start(out[P * n : P * (n + 1), :], wins[n][:])
 
-        def pick(target, j, g0, g1):
-            nc.vector.tensor_copy(target, planes[j][:].indirect(offs_sb[:, GO * g0 : GO * g1]))
-
-        last = G - 1
-        pick(p01[:, 0, :], 0, 0, last)
-        pick(rows[:, 0, :], 0, last, G)
-        for g in range(last):
-            pick(p01[:, 1, GS * g : GS * (g + 1)], 1, g, g + 1)
-            nc.scalar.copy(x4[g][:, :, 0:2], p01[:, :, GS * g : GS * (g + 1)].rearrange("p t c -> p c t"))
-        pick(rows[:, 1, :], 1, last, G)
-        for j in (2, 3):
-            for g in range(last):
-                pick(p23[g][:, j - 2, :], j, g, g + 1)
-        pick(rows[:, 3, :], 3, last, G)
-        for c in range(2):
-            cols = slice(C * c, C * (c + 1))
-            nc.scalar.copy(x4[0][:, cols, 2:4], p23[0][:, :, cols].rearrange("p t c -> p c t"))
-            quant(0, cols)
-        pick(rows[:, 2, :], 2, last, G)
-        nc.scalar.copy(x4[1][:, :, 2:4], p23[1].rearrange("p t c -> p c t"))
-        x4.append(keep.tile([P, GS, 4], BF16, name="x4_0", align_bytes=64))
-        nc.vector.tensor_copy(
-            x4[last][:].rearrange("p (c i) t -> p c t i", i=4), rows.rearrange("p t (c i) -> p c t i", i=4)
-        )
-        for g in range(1, G):
-            quant(g, slice(0, GS))
-
-        w1_first = keep.tile([P, 2, 2 * H], U8, name="w1_first", align_bytes=64)
-        w3_first = keep.tile([P, 2, 2 * H], U8, name="plane0", align_bytes=64)
-        w13 = [(w1_first[:], w3_first[:])]
-        for g in range(1, G):
-            both = keep.tile([P, 2, 2, 2 * H], U8, name=("plane1", "plane3")[g - 1], align_bytes=64)
-            w13.append((both[:, 0, :, :], both[:, 1, :, :]))
-        w2_sb = keep.tile([P, E, 2 * N], U8, name="plane2", align_bytes=64)
-        gate_sb = keep.tile([P, E * C], F32, name="p01")
-        load_scales(s1_sb, w1_scales)
-        for g in range(G):
-            load_words(w13[g][0], w1_words, 2 * g, 2 * g + 2)
-            load_words(w13[g][1], w3_words, 2 * g, 2 * g + 2)
-            if g == 0:
-                load_scales(s3_sb, w3_scales)
-        load_scales(s2_sb, w2_scales)
-        load_words(w2_sb[:], w2_words, 0, E)
-        nc.sync.dma_start(out=gate_sb[:], in_=gate[0:P, :])
-
-        idle = psum.tile([P, H], F32, name="bank")
-        for i in range(2):
-            nc.tensor.matmul_mx(
-                out=idle[:],
-                lhsT=w1_first[:, 0, 0 : 2 * P].bitcast(FP4X4),
-                lhsT_scale=zs[:, 0:P],
-                rhs=zq[:].bitcast(FP8X4),
-                rhs_scale=zs[:],
-                start=True,
-                stop=True,
-            )
-
-        for s in range(G + 3):
-            if s < G:
-                front(s)
-            if 1 <= s <= G:
-                middle(s - 1)
-            if s >= 3:
-                back(s - 3, 1)
-            if 2 <= s < G + 2:
-                second(s - 2)
-                back(s - 2, 0)
+        for step in range(G + 3):
+            if step < G:
+                hidden(step)
+            if 1 <= step <= G:
+                turn_and_quantise(step - 1)
+            if step >= 3:
+                scatter(step - 3, 1)
+            if 2 <= step < G + 2:
+                second_product(step - 2)
+                scatter(step - 2, 0)

@@ -22,7 +22,6 @@ G = E // 2
 LAST = G - 1
 GS = 2 * C
 GO = GS // 16
-WARM_PASSES = 2
 
 
 def tile_moe_two_glu_sigmoid_kernel(
@@ -41,45 +40,26 @@ def tile_moe_two_glu_sigmoid_kernel(
         ident = keep.tile([P, P], F32, name="ident")
         planes = [keep.tile([P, T], F32, name=f"plane{t}", align_bytes=64) for t in range(4)]
         s1_sb = keep.tile([P, E, H], U8, name="s1_sb", align_bytes=64)
-        s3_sb = keep.tile([P, E, H], U8, name="s3_sb", align_bytes=64)
+        zero_src = keep.tile([P, 1], F32, name="zero_src", align_bytes=64)
         s2_sb = keep.tile([P, E, N], U8, name="s2_sb", align_bytes=64)
         wins = [keep.tile([P, T], F32, name=f"win{n}", align_bytes=64) for n in range(2)]
-        zero_in = keep.tile([P, 4 * H], BF16, name="zero_in", align_bytes=64)
-        zero_codes = keep.tile([P, H], U32, name="zero_codes", align_bytes=64)
-        zero_scales = keep.tile([P, H], U8, name="zero_scales", align_bytes=64)
+        zero_in = keep.tile([P, 4 * P], BF16, name="zero_in", align_bytes=64)
+        zero_codes = keep.tile([P, P], U32, name="zero_codes", align_bytes=64)
+        zero_scales = keep.tile([P, P], U8, name="zero_scales", align_bytes=64)
         p01 = keep.tile([P, 2, LAST * GS], F32, name="p01")
-        five = keep.tile([P, 5, GS], F32, name="five")
-        last_rows = five[:, 1:5, :]
-        p23_1 = keep.tile([P, 2, GS], F32, name="p23_1")
-        p23 = [five[:, 0:4:3, :], p23_1[:]]
+        four = keep.tile([P, 4, GS], F32, name="four")
+        p23 = [keep.tile([P, 2, GS], F32, name=f"p23_{g}")[:] for g in range(LAST)]
         x4 = [keep.tile([P, GS, 4], BF16, name=f"x4_{g}", align_bytes=64) for g in range(LAST)]
         xq = [keep.tile([P, GS], U32, name=f"xq_{g}", align_bytes=64) for g in range(G)]
         xs = [keep.tile([P, GS], U8, name=f"xs_{g}", align_bytes=64) for g in range(G)]
 
-        x_rows = xT.rearrange("(p t) j -> p t j", t=4)
-        for t in range(4):
-            nc.sync.dma_start(out=planes[t][:], in_=x_rows[:, t, :])
-            if t == 0:
-                nc.sync.dma_start(offs_sb[:], offs)
-                nc.sync.dma_start(dst_sb[:], dst)
-
-        nc.vector.memset(zero[:], 0.0)
-        nc.scalar.activation(warm[:], zero[:], ACT.Sigmoid)
-        for scales_sb in (s1_sb, s3_sb, s2_sb):
-            nc.vector.memset(scales_sb[:].rearrange("p e i -> p (e i)").bitcast(I32), 0)
-        nc.scalar.copy(zero_in[:].bitcast(F32), zero[:].to_broadcast([P, 2 * H]))
-        nc.vector.quantize_mx(out=zero_codes[:].bitcast(FP8X4), scales=zero_scales[:], in_=zero_in[:])
-        for win in wins:
-            nc.scalar.copy(win[:], zero[:].to_broadcast([P, T]))
-        make_identity(nc, ident[:])
-
-        def load_scales(scales_sb, dram):
+        def load_scales(scales_sb, dram, e0, e1):
             flat = scales_sb[:].rearrange("p e i -> p (e i)").bitcast(I32)
             width = scales_sb.shape[2] // 4
             for r in range(4):
                 nc.sync.dma_start(
-                    out=flat[r:P:32, :].rearrange("q (e i) -> q e i", i=width),
-                    in_=dram[:, 0, r:16:4, :].rearrange("e q i -> q e i").bitcast(I32),
+                    out=flat[r:P:32, width * e0 : width * e1].rearrange("q (e i) -> q e i", i=width),
+                    in_=dram[e0:e1, 0, r:16:4, :].rearrange("e q i -> q e i").bitcast(I32),
                 )
 
         def load_words(view, dram, e0, e1):
@@ -87,6 +67,48 @@ def tile_moe_two_glu_sigmoid_kernel(
                 out=view.bitcast(I32),
                 in_=dram[e0:e1, 0, :, :].rearrange("e p b -> p e b").bitcast(I32),
             )
+
+        gate_rows = keep.tile([P, C], F32, name="gate_rows")
+        gate_col = keep.tile([P, E], F32, name="gate_col")
+        nc.gpsimd.memset(gate_rows[:], 0.0)
+        gate_sb = keep.tile([P, E * C], F32, name="gate_sb")
+        x_rows = xT.rearrange("(p t) j -> p t j", t=4)
+        for t in range(4):
+            nc.sync.dma_start(out=planes[t][:], in_=x_rows[:, t, :])
+            if t == 0:
+                nc.sync.dma_start(offs_sb[:], offs)
+                nc.sync.dma_start(dst_sb[:], dst)
+                nc.sync.dma_start(out=gate_rows[0:E, :], in_=gate[0, :].rearrange("(e c) -> e c", c=C))
+        w1_first = keep.tile([P, 2, 2 * H], U8, name="w1_first", align_bytes=64)
+        w1_sb = [w1_first[:]]
+        load_words(w1_sb[0], w1_words, 0, 2)
+
+        nc.vector.memset(zero[:], 0.0)
+        nc.scalar.activation(warm[:], zero[:], ACT.Sigmoid)
+        for scales_sb in (s1_sb, s2_sb):
+            nc.vector.memset(scales_sb[:].rearrange("p e i -> p (e i)").bitcast(I32), 0)
+        load_scales(s1_sb, w1_scales, 0, E)
+        nc.vector.memset(zero_src[:], 0.0)
+        nc.scalar.copy(zero_in[:].bitcast(F32), zero_src[:].to_broadcast([P, 2 * P]))
+        nc.vector.quantize_mx(out=zero_codes[:].bitcast(FP8X4), scales=zero_scales[:], in_=zero_in[:])
+        w3_first = keep.tile([P, 2, 2 * H], U8, name="w3_first", tag="zero_in", align_bytes=64)
+        w3_sb = [w3_first[:]]
+        load_words(w3_sb[0], w3_words, 0, 2)
+        s3_sb = keep.tile([P, E, H], U8, name="s3_sb", tag="zero_src", align_bytes=64)
+        nc.vector.memset(s3_sb[:].rearrange("p e i -> p (e i)").bitcast(I32), 0)
+        load_scales(s3_sb, w3_scales, 0, E)
+        for win in wins:
+            nc.scalar.copy(win[:], zero[:].to_broadcast([P, T]))
+        make_identity(nc, ident[:])
+        turned_gate = psum.tile([P, P], F32, name="bank")
+        nc.tensor.transpose(turned_gate[:], gate_rows[:], ident[:])
+        nc.scalar.copy(gate_col[:], turned_gate[:, 0:E])
+        for half in range(2):
+            spread = psum.tile([P, E // 2, C], F32, name="bank")
+            for j in range(E // 2):
+                e = half * (E // 2) + j
+                nc.tensor.transpose(spread[:, j, :], gate_col[:, e : e + 1].to_broadcast([P, P]), ident[:])
+            nc.scalar.copy(gate_sb[:, half * 3 * C : (half + 1) * 3 * C], spread[:].rearrange("p j c -> p (j c)"))
 
         def gather(target, t, g0, g1):
             nc.vector.tensor_copy(target, planes[t][:].indirect(offs_sb[:, GO * g0 : GO * g1]))
@@ -99,58 +121,53 @@ def tile_moe_two_glu_sigmoid_kernel(
             )
 
         gather(p01[:, 0, :], 0, 0, LAST)
-        gather(last_rows[:, 0, :], 0, LAST, G)
+        gather(four[:, 0, :], 0, LAST, G)
+        w13_1 = keep.tile([P, 2, 2, 2 * H], U8, name="w13_1", tag="plane0", align_bytes=64)
+        w1_sb.append(w13_1[:, 0, :, :])
+        w3_sb.append(w13_1[:, 1, :, :])
+        load_words(w1_sb[1], w1_words, 2, 4)
+        load_words(w3_sb[1], w3_words, 2, 4)
+
+        unread = psum.tile([P, H], F32, name="bank")
+        for i in range(2):
+            nc.tensor.matmul_mx(
+                out=unread[:],
+                lhsT=zero_codes[:].bitcast(FP8X4),
+                lhsT_scale=zero_scales[:],
+                rhs=w1_sb[0][:, 0, :].bitcast(FP4X4),
+                rhs_scale=s2_sb[:, 0:2, :].rearrange("p e n -> p (e n)"),
+                start=True,
+                stop=True,
+            )
+        load_scales(s2_sb, w2_scales, 0, E)
+
         for g in range(LAST):
             gather(p01[:, 1, GS * g : GS * (g + 1)], 1, g, g + 1)
             nc.scalar.copy(x4[g][:, :, 0:2], p01[:, :, GS * g : GS * (g + 1)].rearrange("p t c -> p c t"))
-        gather(last_rows[:, 1, :], 1, LAST, G)
+        gather(four[:, 1, :], 1, LAST, G)
         for t in (2, 3):
             for g in range(LAST):
                 gather(p23[g][:, t - 2, :], t, g, g + 1)
-        gather(last_rows[:, 3, :], 3, LAST, G)
+            gather(four[:, t, :], t, LAST, G)
         for c in range(2):
             cols = slice(C * c, C * (c + 1))
             nc.scalar.copy(x4[0][:, cols, 2:4], p23[0][:, :, cols].rearrange("p t c -> p c t"))
             quantise_x(0, cols)
-        gather(last_rows[:, 2, :], 2, LAST, G)
         nc.scalar.copy(x4[1][:, :, 2:4], p23[1].rearrange("p t c -> p c t"))
+        quantise_x(1, slice(0, GS))
+
         x4.append(keep.tile([P, GS, 4], BF16, name="x4_last", tag="x4_0", align_bytes=64))
         nc.vector.tensor_copy(
-            x4[LAST][:].rearrange("p (c i) t -> p c t i", i=4), last_rows.rearrange("p t (c i) -> p c t i", i=4)
+            x4[LAST][:].rearrange("p (c i) t -> p c t i", i=4), four[:].rearrange("p t (c i) -> p c t i", i=4)
         )
-        for g in range(1, G):
-            quantise_x(g, slice(0, GS))
-
-        w1_first = keep.tile([P, 2, 2 * H], U8, name="w1_first", align_bytes=64)
-        w3_first = keep.tile([P, 2, 2 * H], U8, name="w3_first", tag="plane0", align_bytes=64)
-        w13_1 = keep.tile([P, 2, 2, 2 * H], U8, name="w13_1", tag="plane1", align_bytes=64)
-        w13_2 = keep.tile([P, 2, 2, 2 * H], U8, name="w13_2", tag="plane3", align_bytes=64)
-        w1_sb = [w1_first[:], w13_1[:, 0, :, :], w13_2[:, 0, :, :]]
-        w3_sb = [w3_first[:], w13_1[:, 1, :, :], w13_2[:, 1, :, :]]
-        w2_sb = keep.tile([P, E, 2 * N], U8, name="w2_sb", tag="plane2", align_bytes=64)
-        gate_sb = keep.tile([P, E * C], F32, name="gate_sb", tag="p01")
-        load_scales(s1_sb, w1_scales)
-        for g in range(G):
-            load_words(w1_sb[g], w1_words, 2 * g, 2 * g + 2)
-            load_words(w3_sb[g], w3_words, 2 * g, 2 * g + 2)
-            if g == 0:
-                load_scales(s3_sb, w3_scales)
-        load_scales(s2_sb, w2_scales)
-        for e0, e1 in ((0, 2), (2, E)):
-            load_words(w2_sb[:, e0:e1, :], w2_words, e0, e1)
-            nc.sync.dma_start(out=gate_sb[:, C * e0 : C * e1], in_=gate[0:P, C * e0 : C * e1])
-
-        unread = psum.tile([P, H], F32, name="bank")
-        for i in range(WARM_PASSES):
-            nc.tensor.matmul_mx(
-                out=unread[:],
-                lhsT=w1_first[:, 0, 0 : 2 * P].bitcast(FP4X4),
-                lhsT_scale=zero_scales[:, 0:P],
-                rhs=zero_codes[:].bitcast(FP8X4),
-                rhs_scale=zero_scales[:],
-                start=True,
-                stop=True,
-            )
+        quantise_x(LAST, slice(0, GS))
+        late = keep.tile([P, 5, 2 * H], U8, name="late", tag="plane3", align_bytes=64)
+        w2_first = late[:, 4, :].rearrange("p (e b) -> p e b", e=2)
+        w1_sb.append(late[:, 0:2, :])
+        w3_sb.append(late[:, 2:4, :])
+        load_words(w1_sb[2], w1_words, 4, 6)
+        load_words(w3_sb[2], w3_words, 4, 6)
+        load_words(w2_first, w2_words, 0, 2)
 
         hid, h_codes, y_banks = {}, {}, {}
 
@@ -177,9 +194,9 @@ def tile_moe_two_glu_sigmoid_kernel(
             a = [first_product(e, w1_sb, s1_sb) for e in pair]
             b = [first_product(e, w3_sb, s3_sb) for e in pair]
             for c, e in enumerate(pair):
-                sg = keep.tile([P, 2, P, 2], F32, name=f"sg{e}")
+                sg = keep.tile([P, 2, P, 2], F32, name=f"sg{e}", align_bytes=64)
                 nc.scalar.activation(sg[:], by_half(a[c]), ACT.Sigmoid)
-                h = keep.tile([P, 2, P, 2], BF16, name=f"h{e}")
+                h = keep.tile([P, 2, P, 2], BF16, name=f"h{e}", align_bytes=64)
                 nc.vector.tensor_tensor(h[:], by_half(b[c]), sg[:], MULT)
                 hid[e] = h
 
@@ -200,7 +217,7 @@ def tile_moe_two_glu_sigmoid_kernel(
             nc.vector.quantize_mx(out=hq[:].bitcast(FP8X4), scales=hs[:], in_=h4_flat)
             h_codes[g] = (hq, hs)
 
-        def second_product(g):
+        def second_product(g, w2_pair):
             hq, hs = h_codes[g]
             for n in range(2):
                 y = psum.tile([P, GS], F32, name="bank")
@@ -209,7 +226,7 @@ def tile_moe_two_glu_sigmoid_kernel(
                     cols = slice(C * c, C * (c + 1))
                     nc.tensor.matmul_mx(
                         out=y[:, cols],
-                        lhsT=w2_sb[:, 2 * g + c, 2 * P * n : 2 * P * (n + 1)].bitcast(FP4X4),
+                        lhsT=w2_pair[:, c, 2 * P * n : 2 * P * (n + 1)].bitcast(FP4X4),
                         lhsT_scale=s2_sb[:, 2 * g + c, P * n : P * (n + 1)],
                         rhs=hq[:, cols].bitcast(FP8X4),
                         rhs_scale=hs[:, cols],
@@ -217,26 +234,26 @@ def tile_moe_two_glu_sigmoid_kernel(
                         stop=True,
                     )
 
-        def scatter(g, n):
-            host = 2 * g if n == 0 else E - 1 - 2 * g
-            y_sb = keep.tile([P, GS], F32, name=f"y{g}{n}", tag=f"h{host}")
-            nc.scalar.copy(y_sb[:], y_banks[g, n][:])
-            nc.vector.tensor_tensor(
-                wins[n][:].indirect(dst_sb[:, GO * g : GO * (g + 1)]),
-                y_sb[:],
-                gate_sb[:, GS * g : GS * (g + 1)],
-                MULT,
-            )
-            if g == LAST:
+        def scatter(n, g0, g1, y_sb, gates):
+            for g in range(g0, g1):
+                nc.scalar.copy(y_sb[:, GS * (g - g0) : GS * (g - g0 + 1)], y_banks[g, n][:])
+            nc.vector.tensor_tensor(wins[n][:].indirect(dst_sb[:, GO * g0 : GO * g1]), y_sb[:], gates, MULT)
+            if g1 == G:
                 nc.sync.dma_start(out[P * n : P * (n + 1), :], wins[n][:])
 
-        for step in range(G + 3):
-            if step < G:
-                hidden(step)
-            if 1 <= step <= G:
-                turn_and_quantise(step - 1)
-            if step >= 3:
-                scatter(step - 3, 1)
-            if 2 <= step < G + 2:
-                second_product(step - 2)
-                scatter(step - 2, 0)
+        hidden(0)
+        w2_rest = keep.tile([P, E - 2, 2 * N], U8, name="w2_rest", tag="sg0", align_bytes=64)
+        load_words(w2_rest[:], w2_words, 2, E)
+        hidden(1)
+        turn_and_quantise(0)
+        hidden(2)
+        turn_and_quantise(1)
+        second_product(0, w2_first)
+        scatter(0, 0, 1, keep.tile([P, GS], F32, name="y00"), gate_sb[:, 0:GS])
+        turn_and_quantise(2)
+        second_product(1, w2_rest[:, 0:2, :])
+        scatter(0, 1, 2, keep.tile([P, GS], F32, name="y10"), gate_sb[:, GS : 2 * GS])
+        scatter(1, 0, 1, keep.tile([P, GS], F32, name="y01", tag="h5", align_bytes=64), gate_sb[:, 0:GS])
+        second_product(2, w2_rest[:, 2:4, :])
+        scatter(0, 2, 3, keep.tile([P, GS], F32, name="y20"), gate_sb[:, 2 * GS : 3 * GS])
+        scatter(1, 1, 3, keep.tile([P, 2 * GS], F32, name="y_rest"), gate_sb[:, GS : 3 * GS])

@@ -40,12 +40,12 @@ def tile_moe_two_glu_sigmoid_kernel(
         ident = keep.tile([P, P], F32, name="ident")
         planes = [keep.tile([P, T], F32, name=f"plane{t}", align_bytes=64) for t in range(4)]
         s1_sb = keep.tile([P, E, H], U8, name="s1_sb", align_bytes=64)
-        zero_src = keep.tile([P, 1], F32, name="zero_src", align_bytes=64)
         s2_sb = keep.tile([P, E, N], U8, name="s2_sb", align_bytes=64)
         wins = [keep.tile([P, T], F32, name=f"win{n}", align_bytes=64) for n in range(2)]
-        zero_in = keep.tile([P, 4 * P], BF16, name="zero_in", align_bytes=64)
-        zero_codes = keep.tile([P, P], U32, name="zero_codes", align_bytes=64)
-        zero_scales = keep.tile([P, P], U8, name="zero_scales", align_bytes=64)
+        warm_in = keep.tile([P, 4 * P], BF16, name="warm_in", align_bytes=64)
+        warm_codes = keep.tile([P, P], U32, name="warm_codes", align_bytes=64)
+        warm_scales = keep.tile([P, P], U8, name="warm_scales", align_bytes=64)
+        warm_wide = keep.tile([P, H], U8, name="warm_wide", align_bytes=64)
         p01 = keep.tile([P, 2, LAST * GS], F32, name="p01")
         four = keep.tile([P, 4, GS], F32, name="four")
         p23 = [keep.tile([P, 2, GS], F32, name=f"p23_{g}")[:] for g in range(LAST)]
@@ -74,7 +74,11 @@ def tile_moe_two_glu_sigmoid_kernel(
         gate_sb = keep.tile([P, E * C], F32, name="gate_sb")
         x_rows = xT.rearrange("(p t) j -> p t j", t=4)
         for t in range(4):
-            nc.sync.dma_start(out=planes[t][:], in_=x_rows[:, t, :])
+            if t == 0:
+                nc.sync.dma_start(out=planes[0][:, 0 : 4 * C], in_=x_rows[:, 0, 0 : 4 * C])
+                nc.sync.dma_start(out=planes[0][:, 4 * C : T], in_=x_rows[:, 0, 4 * C : T])
+            else:
+                nc.sync.dma_start(out=planes[t][:], in_=x_rows[:, t, :])
             if t == 0:
                 nc.sync.dma_start(offs_sb[:], offs)
                 nc.sync.dma_start(dst_sb[:], dst)
@@ -88,15 +92,18 @@ def tile_moe_two_glu_sigmoid_kernel(
         for scales_sb in (s1_sb, s2_sb):
             nc.vector.memset(scales_sb[:].rearrange("p e i -> p (e i)").bitcast(I32), 0)
         load_scales(s1_sb, w1_scales, 0, E)
-        nc.vector.memset(zero_src[:], 0.0)
-        nc.scalar.copy(zero_in[:].bitcast(F32), zero_src[:].to_broadcast([P, 2 * P]))
-        nc.vector.quantize_mx(out=zero_codes[:].bitcast(FP8X4), scales=zero_scales[:], in_=zero_in[:])
-        w3_first = keep.tile([P, 2, 2 * H], U8, name="w3_first", tag="zero_in", align_bytes=64)
+        w3_first = keep.tile([P, 2, 2 * H], U8, name="w3_first", align_bytes=64)
         w3_sb = [w3_first[:]]
         load_words(w3_sb[0], w3_words, 0, 2)
-        s3_sb = keep.tile([P, E, H], U8, name="s3_sb", tag="zero_src", align_bytes=64)
+        s3_sb = keep.tile([P, E, H], U8, name="s3_sb", align_bytes=64)
         nc.vector.memset(s3_sb[:].rearrange("p e i -> p (e i)").bitcast(I32), 0)
         load_scales(s3_sb, w3_scales, 0, E)
+        nc.vector.tensor_copy(warm_in[:], planes[0][:, 0 : 4 * C])
+        nc.vector.quantize_mx(out=warm_codes[:].bitcast(FP8X4), scales=warm_scales[:], in_=warm_in[:])
+        nc.vector.tensor_copy(
+            warm_wide[:].bitcast(I32).rearrange("p (r c) -> p r c", r=4),
+            warm_scales[:].bitcast(I32).unsqueeze(1).to_broadcast([P, 4, P // 4]),
+        )
         for win in wins:
             nc.scalar.copy(win[:], zero[:].to_broadcast([P, T]))
         make_identity(nc, ident[:])
@@ -132,10 +139,10 @@ def tile_moe_two_glu_sigmoid_kernel(
         for i in range(2):
             nc.tensor.matmul_mx(
                 out=unread[:],
-                lhsT=zero_codes[:].bitcast(FP8X4),
-                lhsT_scale=zero_scales[:],
+                lhsT=warm_codes[:].bitcast(FP8X4),
+                lhsT_scale=warm_scales[:],
                 rhs=w1_sb[0][:, 0, :].bitcast(FP4X4),
-                rhs_scale=s2_sb[:, 0:2, :].rearrange("p e n -> p (e n)"),
+                rhs_scale=warm_wide[:],
                 start=True,
                 stop=True,
             )

@@ -146,7 +146,6 @@ def tile_moe_two_glu_sigmoid_kernel(
                 start=True,
                 stop=True,
             )
-        load_scales(s2_sb, w2_scales, 0, E)
 
         for g in range(LAST):
             gather(p01[:, 1, GS * g : GS * (g + 1)], 1, g, g + 1)
@@ -174,6 +173,7 @@ def tile_moe_two_glu_sigmoid_kernel(
         w3_sb.append(late[:, 2:4, :])
         load_words(w1_sb[2], w1_words, 4, 6)
         load_words(w3_sb[2], w3_words, 4, 6)
+        load_scales(s2_sb, w2_scales, 0, E)
         load_words(w2_first, w2_words, 0, 2)
 
         hid, h_codes, y_banks = {}, {}, {}

@@ -75,12 +75,12 @@ def tile_moe_two_glu_sigmoid_kernel(
         x_rows = xT.rearrange("(p t) j -> p t j", t=4)
         for t in range(4):
             if t == 0:
-                nc.sync.dma_start(out=planes[0][:, 0 : 4 * C], in_=x_rows[:, 0, 0 : 4 * C])
-                nc.sync.dma_start(out=planes[0][:, 4 * C : T], in_=x_rows[:, 0, 4 * C : T])
+                nc.sync.dma_start(out=planes[0][:, 0:GS], in_=x_rows[:, 0, 0:GS])
+                nc.sync.dma_start(offs_sb[:], offs)
+                nc.sync.dma_start(out=planes[0][:, GS:T], in_=x_rows[:, 0, GS:T])
             else:
                 nc.sync.dma_start(out=planes[t][:], in_=x_rows[:, t, :])
             if t == 0:
-                nc.sync.dma_start(offs_sb[:], offs)
                 nc.sync.dma_start(dst_sb[:], dst)
                 nc.sync.dma_start(out=gate_rows[0:E, :], in_=gate[0, :].rearrange("(e c) -> e c", c=C))
         w1_first = keep.tile([P, 2, 2 * H], U8, name="w1_first", align_bytes=64)
@@ -98,7 +98,9 @@ def tile_moe_two_glu_sigmoid_kernel(
         s3_sb = keep.tile([P, E, H], U8, name="s3_sb", align_bytes=64)
         nc.vector.memset(s3_sb[:].rearrange("p e i -> p (e i)").bitcast(I32), 0)
         load_scales(s3_sb, w3_scales, 0, E)
-        nc.vector.tensor_copy(warm_in[:], planes[0][:, 0 : 4 * C])
+        nc.vector.tensor_copy(
+            warm_in[:].rearrange("p (r c) -> p r c", r=2), planes[0][:, 0:GS].unsqueeze(1).to_broadcast([P, 2, GS])
+        )
         nc.vector.quantize_mx(out=warm_codes[:].bitcast(FP8X4), scales=warm_scales[:], in_=warm_in[:])
         nc.vector.tensor_copy(
             warm_wide[:].bitcast(I32).rearrange("p (r c) -> p r c", r=4),
@@ -254,13 +256,12 @@ def tile_moe_two_glu_sigmoid_kernel(
         hidden(1)
         turn_and_quantise(0)
         hidden(2)
-        turn_and_quantise(1)
         second_product(0, w2_first)
         scatter(0, 0, 1, keep.tile([P, GS], F32, name="y00"), gate_sb[:, 0:GS])
+        turn_and_quantise(1)
         turn_and_quantise(2)
-        second_product(1, w2_rest[:, 0:2, :])
-        scatter(0, 1, 2, keep.tile([P, GS], F32, name="y10"), gate_sb[:, GS : 2 * GS])
         scatter(1, 0, 1, keep.tile([P, GS], F32, name="y01", tag="h5", align_bytes=64), gate_sb[:, 0:GS])
+        second_product(1, w2_rest[:, 0:2, :])
         second_product(2, w2_rest[:, 2:4, :])
-        scatter(0, 2, 3, keep.tile([P, GS], F32, name="y20"), gate_sb[:, 2 * GS : 3 * GS])
-        scatter(1, 1, 3, keep.tile([P, 2 * GS], F32, name="y_rest"), gate_sb[:, GS : 3 * GS])
+        for n in range(2):
+            scatter(n, 1, G, keep.tile([P, 2 * GS], F32, name=f"y_rest{n}"), gate_sb[:, GS : G * GS])

@@ -19,7 +19,6 @@ MULT = mybir.AluOpType.mult
 
 P = 128
 G = E // 2
-LAST = G - 1
 GS = 2 * C
 GO = GS // 16
 
@@ -30,160 +29,161 @@ def tile_moe_two_glu_sigmoid_kernel(
     nc = tc.nc
     with ExitStack() as ctx:
         keep = ctx.enter_context(tc.tile_pool(name="keep", bufs=1))
-        work = ctx.enter_context(tc.tile_pool(name="work", bufs=G))
-        psum = ctx.enter_context(tc.psum_pool(name="psum", bufs=8))
+        psum = ctx.enter_context(tc.psum_pool(name="psum", bufs=1))
 
-        offs_sb = keep.tile([P, E * C // 16], U16, name="offs_sb")
-        dst_sb = keep.tile([P, E * C // 16], U16, name="dst_sb")
-        zero = keep.tile([P, 1], F32, name="zero")
-        warm = keep.tile([P, 1], F32, name="warm")
-        ident = keep.tile([P, P], F32, name="ident")
-        planes = [keep.tile([P, T], F32, name=f"plane{t}", align_bytes=64) for t in range(4)]
-        s1_sb = keep.tile([P, E, H], U8, name="s1_sb", align_bytes=64)
-        s2_sb = keep.tile([P, E, N], U8, name="s2_sb", align_bytes=64)
-        wins = [keep.tile([P, T], F32, name=f"win{n}", align_bytes=64) for n in range(2)]
-        warm_in = keep.tile([P, 4 * P], BF16, name="warm_in", align_bytes=64)
-        warm_codes = keep.tile([P, P], U32, name="warm_codes", align_bytes=64)
-        warm_scales = keep.tile([P, P], U8, name="warm_scales", align_bytes=64)
-        warm_wide = keep.tile([P, H], U8, name="warm_wide", align_bytes=64)
-        p01 = keep.tile([P, 2, LAST * GS], F32, name="p01")
-        four = keep.tile([P, 4, GS], F32, name="four")
-        p23 = [keep.tile([P, 2, GS], F32, name=f"p23_{g}")[:] for g in range(LAST)]
-        x4 = [keep.tile([P, GS, 4], BF16, name=f"x4_{g}", align_bytes=64) for g in range(LAST)]
-        xq = [keep.tile([P, GS], U32, name=f"xq_{g}", align_bytes=64) for g in range(G)]
-        xs = [keep.tile([P, GS], U8, name=f"xs_{g}", align_bytes=64) for g in range(G)]
+        def tile(shape, dtype, name, tag=None):
+            return keep.tile(shape, dtype, name=name, tag=tag or name, align_bytes=64)
 
-        def load_scales(scales_sb, dram, e0, e1):
+        def bank(b, shape, name):
+            return psum.tile(shape, F32, name=name, tag=f"bank{b}")
+
+        offs_sb = tile([P, E * C // 16], U16, "offs_sb")
+        dst_sb = tile([P, E * C // 16], U16, "dst_sb")
+        ident = tile([P, P], F32, "ident")
+        planes = [tile([P, T], F32, f"plane{t}") for t in range(4)]
+        wins = [tile([P, T], F32, f"win{n}") for n in range(2)]
+        gate_rows = tile([P, C], F32, "gate_rows")
+        s1_sb = tile([P, E, H], U8, "s1_sb")
+        s3_sb = tile([P, E, H], U8, "s3_sb")
+        s2_sb = tile([P, E, N], U8, "s2_sb")
+        w1_sb = [tile([P, 2, 2 * H], U8, f"w1_{g}") for g in range(G)]
+        w3_sb = [tile([P, 2, 2 * H], U8, f"w3_{g}") for g in range(G)]
+        w2_first = tile([P, 2, 2 * N], U8, "w2_first")
+        w2_rest = tile([P, E - 2, 2 * N], U8, "w2_rest")
+        w2_sb = [w2_first[:], w2_rest[:, 0:2, :], w2_rest[:, 2:4, :]]
+
+        def load_scales(scales_sb, dram):
             flat = scales_sb[:].rearrange("p e i -> p (e i)").bitcast(I32)
             width = scales_sb.shape[2] // 4
             for r in range(4):
                 nc.sync.dma_start(
-                    out=flat[r:P:32, width * e0 : width * e1].rearrange("q (e i) -> q e i", i=width),
-                    in_=dram[e0:e1, 0, r:16:4, :].rearrange("e q i -> q e i").bitcast(I32),
+                    out=flat[r:P:32, :].rearrange("q (e i) -> q e i", i=width),
+                    in_=dram[:, 0, r:16:4, :].rearrange("e q i -> q e i").bitcast(I32),
                 )
 
-        def load_words(view, dram, e0, e1):
+        def load_words(words_sb, dram, e0, e1):
             nc.sync.dma_start(
-                out=view.bitcast(I32),
+                out=words_sb[:].bitcast(I32),
                 in_=dram[e0:e1, 0, :, :].rearrange("e p b -> p e b").bitcast(I32),
             )
 
-        gate_rows = keep.tile([P, C], F32, name="gate_rows")
-        gate_col = keep.tile([P, E], F32, name="gate_col")
         nc.gpsimd.memset(gate_rows[:], 0.0)
-        gate_sb = keep.tile([P, E * C], F32, name="gate_sb")
         x_rows = xT.rearrange("(p t) j -> p t j", t=4)
-        for t in range(4):
-            if t == 0:
-                nc.sync.dma_start(out=planes[0][:, 0:GS], in_=x_rows[:, 0, 0:GS])
-                nc.sync.dma_start(offs_sb[:], offs)
-                nc.sync.dma_start(out=planes[0][:, GS:T], in_=x_rows[:, 0, GS:T])
-            else:
-                nc.sync.dma_start(out=planes[t][:], in_=x_rows[:, t, :])
-            if t == 0:
-                nc.sync.dma_start(dst_sb[:], dst)
-                nc.sync.dma_start(out=gate_rows[0:E, :], in_=gate[0, :].rearrange("(e c) -> e c", c=C))
-        w1_first = keep.tile([P, 2, 2 * H], U8, name="w1_first", align_bytes=64)
-        w1_sb = [w1_first[:]]
+        nc.sync.dma_start(out=planes[0][:], in_=x_rows[:, 0, :])
+        nc.sync.dma_start(offs_sb[:], offs)
+        nc.sync.dma_start(out=gate_rows[0:E, :], in_=gate[0, :].rearrange("(e c) -> e c", c=C))
+        for t in range(1, 4):
+            nc.sync.dma_start(out=planes[t][:], in_=x_rows[:, t, :])
         load_words(w1_sb[0], w1_words, 0, 2)
-
-        nc.vector.memset(zero[:], 0.0)
-        nc.scalar.activation(warm[:], zero[:], ACT.Sigmoid)
-        for scales_sb in (s1_sb, s2_sb):
-            nc.vector.memset(scales_sb[:].rearrange("p e i -> p (e i)").bitcast(I32), 0)
-        load_scales(s1_sb, w1_scales, 0, E)
-        w3_first = keep.tile([P, 2, 2 * H], U8, name="w3_first", align_bytes=64)
-        w3_sb = [w3_first[:]]
+        load_scales(s1_sb, w1_scales)
         load_words(w3_sb[0], w3_words, 0, 2)
-        s3_sb = keep.tile([P, E, H], U8, name="s3_sb", align_bytes=64)
-        nc.vector.memset(s3_sb[:].rearrange("p e i -> p (e i)").bitcast(I32), 0)
-        load_scales(s3_sb, w3_scales, 0, E)
-        nc.vector.tensor_copy(
-            warm_in[:].rearrange("p (r c) -> p r c", r=2), planes[0][:, 0:GS].unsqueeze(1).to_broadcast([P, 2, GS])
-        )
-        nc.vector.quantize_mx(out=warm_codes[:].bitcast(FP8X4), scales=warm_scales[:], in_=warm_in[:])
-        nc.vector.tensor_copy(
-            warm_wide[:].bitcast(I32).rearrange("p (r c) -> p r c", r=4),
-            warm_scales[:].bitcast(I32).unsqueeze(1).to_broadcast([P, 4, P // 4]),
-        )
-        for win in wins:
-            nc.scalar.copy(win[:], zero[:].to_broadcast([P, T]))
+        load_scales(s3_sb, w3_scales)
+        load_words(w1_sb[1], w1_words, 2, 4)
+        load_words(w3_sb[1], w3_words, 2, 4)
+        load_scales(s2_sb, w2_scales)
+        load_words(w1_sb[2], w1_words, 4, 6)
+        load_words(w3_sb[2], w3_words, 4, 6)
+        load_words(w2_first, w2_words, 0, 2)
+        nc.sync.dma_start(dst_sb[:], dst)
+        load_words(w2_rest, w2_words, 2, E)
+
+        warm = tile([P, 2], F32, "warm")
+        nc.vector.memset(warm[:, 0:1], 0.0)
+        nc.scalar.activation(warm[:, 1:2], warm[:, 0:1], ACT.Sigmoid)
         make_identity(nc, ident[:])
-        turned_gate = psum.tile([P, P], F32, name="bank")
-        nc.tensor.transpose(turned_gate[:], gate_rows[:], ident[:])
-        nc.scalar.copy(gate_col[:], turned_gate[:, 0:E])
-        for half in range(2):
-            spread = psum.tile([P, E // 2, C], F32, name="bank")
-            for j in range(E // 2):
-                e = half * (E // 2) + j
-                nc.tensor.transpose(spread[:, j, :], gate_col[:, e : e + 1].to_broadcast([P, P]), ident[:])
-            nc.scalar.copy(gate_sb[:, half * 3 * C : (half + 1) * 3 * C], spread[:].rearrange("p j c -> p (j c)"))
+        for win in wins:
+            nc.vector.memset(win[:], 0.0)
 
-        def gather(target, t, g0, g1):
-            nc.vector.tensor_copy(target, planes[t][:].indirect(offs_sb[:, GO * g0 : GO * g1]))
+        first = {0: tile([P, 2, GS], BF16, "first01")}
+        rest = {t: tile([P, 2, 2 * GS], BF16, f"rest{t}") for t in (0, 2)}
+        x4 = [tile([P, GS, 4], BF16, f"x4_{g}") for g in range(G)]
+        xq = [tile([P, GS], U32, f"xq_{g}") for g in range(G)]
+        xs = [tile([P, GS], U8, f"xs_{g}") for g in range(G)]
 
-        def quantise_x(g, cols):
+        def gather_vector(t, c0=0, c1=2):
+            nc.vector.tensor_copy(
+                first[t - t % 2][:, t % 2, C * c0 : C * c1], planes[t][:].indirect(offs_sb[:, GO * c0 // 2 : GO * c1 // 2])
+            )
+
+        def gather_scalar(t, g0, g1):
+            nc.scalar.activation(
+                rest[t - t % 2][:, t % 2, GS * (g0 - 1) : GS * (g1 - 1)],
+                planes[t][:].indirect(offs_sb[:, GO * g0 : GO * g1]),
+                ACT.Copy,
+            )
+
+        def weave(copy, g, t, cols=slice(0, GS)):
+            rows = first[t][:] if g == 0 else rest[t][:, :, GS * (g - 1) : GS * g]
+            copy(x4[g][:, cols, t : t + 2], rows[:, :, cols].rearrange("p t c -> p c t"))
+
+        def quantise_x(g, cols=slice(0, GS)):
             nc.vector.quantize_mx(
                 out=xq[g][:, cols].bitcast(FP8X4),
                 scales=xs[g][:, cols],
                 in_=x4[g][:, cols, :].rearrange("p c t -> p (c t)"),
             )
 
-        gather(p01[:, 0, :], 0, 0, LAST)
-        gather(four[:, 0, :], 0, LAST, G)
-        w13_1 = keep.tile([P, 2, 2, 2 * H], U8, name="w13_1", tag="plane0", align_bytes=64)
-        w1_sb.append(w13_1[:, 0, :, :])
-        w3_sb.append(w13_1[:, 1, :, :])
-        load_words(w1_sb[1], w1_words, 2, 4)
-        load_words(w3_sb[1], w3_words, 2, 4)
+        gather_vector(0)
+        gather_scalar(0, 1, G)
+        warm_codes = tile([P, P], U32, "warm_codes")
+        warm_scales = tile([P, P], U8, "warm_scales")
+        warm_wide = tile([P, H], U8, "warm_wide")
+        nc.vector.quantize_mx(out=warm_codes[:].bitcast(FP8X4), scales=warm_scales[:], in_=rest[0][:, 0, :])
+        nc.vector.tensor_copy(
+            warm_wide[:].bitcast(I32).rearrange("p (r c) -> p r c", r=4),
+            warm_scales[:].bitcast(I32).unsqueeze(1).to_broadcast([P, 4, P // 4]),
+        )
+        gather_vector(1)
+        gather_scalar(1, 1, G)
+        for g in range(G):
+            weave(nc.vector.tensor_copy, g, 0)
+        turned_gate = bank(5, [P, P], "turned_gate")
+        nc.tensor.transpose(turned_gate[:], gate_rows[:], ident[:])
+        gate_col = tile([P, E], F32, "gate_col", "rest0")
+        nc.vector.tensor_copy(gate_col[:], turned_gate[:, 0:E])
+        first[2] = tile([P, 2, GS], BF16, "first23", "first01")
+        gather_vector(2)
+        gather_scalar(2, 1, G)
+        gather_vector(3, 0, 1)
+        gather_vector(3, 1, 2)
+        gather_scalar(3, 2, 3)
+        gather_scalar(3, 1, 2)
+        for c in range(2):
+            weave(nc.vector.tensor_copy, 0, 2, slice(C * c, C * (c + 1)))
+        for c in range(2):
+            quantise_x(0, slice(C * c, C * (c + 1)))
+        weave(nc.vector.tensor_copy, 1, 2)
+        weave(nc.scalar.copy, 2, 2)
+        quantise_x(1)
+        quantise_x(2)
+        gate_sb = tile([P, E * C], F32, "gate_sb", "x4_0")
+        for half in range(2):
+            spread = bank(6 + half, [P, 3, C], f"spread{half}")
+            for j in range(3):
+                e = 3 * half + j
+                nc.tensor.transpose(spread[:, j, :], gate_col[:, e : e + 1].to_broadcast([P, P]), ident[:])
+            (nc.vector.tensor_copy, nc.scalar.copy)[half](
+                gate_sb[:, 3 * C * half : 3 * C * (half + 1)], spread[:].rearrange("p j c -> p (j c)")
+            )
 
-        unread = psum.tile([P, H], F32, name="bank")
-        for i in range(2):
+        unread = bank(5, [P, H], "unread")
+        for width in (H, H // 2):
             nc.tensor.matmul_mx(
-                out=unread[:],
+                out=unread[:, 0:width],
                 lhsT=warm_codes[:].bitcast(FP8X4),
                 lhsT_scale=warm_scales[:],
-                rhs=w1_sb[0][:, 0, :].bitcast(FP4X4),
-                rhs_scale=warm_wide[:],
+                rhs=w1_sb[0][:, 0, 0 : 2 * width].bitcast(FP4X4),
+                rhs_scale=warm_wide[:, 0:width],
                 start=True,
                 stop=True,
             )
 
-        for g in range(LAST):
-            gather(p01[:, 1, GS * g : GS * (g + 1)], 1, g, g + 1)
-            nc.scalar.copy(x4[g][:, :, 0:2], p01[:, :, GS * g : GS * (g + 1)].rearrange("p t c -> p c t"))
-        gather(four[:, 1, :], 1, LAST, G)
-        for t in (2, 3):
-            for g in range(LAST):
-                gather(p23[g][:, t - 2, :], t, g, g + 1)
-            gather(four[:, t, :], t, LAST, G)
-        for c in range(2):
-            cols = slice(C * c, C * (c + 1))
-            nc.scalar.copy(x4[0][:, cols, 2:4], p23[0][:, :, cols].rearrange("p t c -> p c t"))
-            quantise_x(0, cols)
-        nc.scalar.copy(x4[1][:, :, 2:4], p23[1].rearrange("p t c -> p c t"))
-        quantise_x(1, slice(0, GS))
+        sg, b_banks, hid, h4, h_codes, y_banks, y_sb = {}, {}, {}, {}, {}, {}, {}
 
-        x4.append(keep.tile([P, GS, 4], BF16, name="x4_last", tag="x4_0", align_bytes=64))
-        nc.vector.tensor_copy(
-            x4[LAST][:].rearrange("p (c i) t -> p c t i", i=4), four[:].rearrange("p t (c i) -> p c t i", i=4)
-        )
-        quantise_x(LAST, slice(0, GS))
-        late = keep.tile([P, 5, 2 * H], U8, name="late", tag="plane3", align_bytes=64)
-        w2_first = late[:, 4, :].rearrange("p (e b) -> p e b", e=2)
-        w1_sb.append(late[:, 0:2, :])
-        w3_sb.append(late[:, 2:4, :])
-        load_words(w1_sb[2], w1_words, 4, 6)
-        load_words(w3_sb[2], w3_words, 4, 6)
-        load_scales(s2_sb, w2_scales, 0, E)
-        load_words(w2_first, w2_words, 0, 2)
-
-        hid, h_codes, y_banks = {}, {}, {}
-
-        def first_product(e, words, scales_sb):
+        def first_product(e, words, scales_sb, b):
             g, c = divmod(e, 2)
             cols = slice(C * c, C * (c + 1))
-            sums = psum.tile([P, H], F32, name="bank")
+            sums = bank(b, [P, H], f"sums{e}_{b}")
             nc.tensor.matmul_mx(
                 out=sums[:],
                 lhsT=xq[g][:, cols].bitcast(FP8X4),
@@ -198,44 +198,49 @@ def tile_moe_two_glu_sigmoid_kernel(
         def by_half(sums):
             return sums[:].rearrange("p (q u d) -> p u q d", u=2, d=2)
 
-        def hidden(g):
+        def first_layer(g, banks):
             pair = (2 * g, 2 * g + 1)
-            a = [first_product(e, w1_sb, s1_sb) for e in pair]
-            b = [first_product(e, w3_sb, s3_sb) for e in pair]
+            a = [first_product(e, w1_sb, s1_sb, banks[c]) for c, e in enumerate(pair)]
             for c, e in enumerate(pair):
-                sg = keep.tile([P, 2, P, 2], F32, name=f"sg{e}", align_bytes=64)
-                nc.scalar.activation(sg[:], by_half(a[c]), ACT.Sigmoid)
-                h = keep.tile([P, 2, P, 2], BF16, name=f"h{e}", align_bytes=64)
-                nc.vector.tensor_tensor(h[:], by_half(b[c]), sg[:], MULT)
-                hid[e] = h
+                b_banks[e] = first_product(e, w3_sb, s3_sb, banks[2 + c])
+            for c, e in enumerate(pair):
+                sg[e] = tile([P, 2, P, 2], F32, f"sg{e}")
+                nc.scalar.activation(sg[e][:], by_half(a[c]), ACT.Sigmoid)
 
-        def turn_and_quantise(g):
-            h4 = work.tile([P, 2, C, 4], BF16, name="h4", align_bytes=64)
-            h4_flat = h4[:].rearrange("p e c t -> p (e c t)")
+        def hidden(e, tag=None):
+            hid[e] = tile([P, 2, P, 2], BF16, f"h{e}", tag)
+            nc.vector.tensor_tensor(hid[e][:], by_half(b_banks[e]), sg[e][:], MULT)
+
+        def turn(g, copy, b):
+            h4[g] = tile([P, 2, C, 4], BF16, f"h4_{g}")
+            turned = bank(b, [P, 2, 2, C], f"turned{g}")
             for c in range(2):
-                turned = psum.tile([P, 2, C], F32, name="bank")
                 pairs = hid[2 * g + c][:].rearrange("p u q d -> p (u q d)").bitcast(F32)
                 for u in range(2):
-                    nc.tensor.transpose(turned[:, u, :], pairs[:, P * u : P * (u + 1)], ident[:])
-                nc.scalar.copy(
-                    h4_flat.bitcast(F32)[:, 2 * C * c : 2 * C * (c + 1)].rearrange("p (c u) -> p c u", u=2),
-                    turned[:].rearrange("p u c -> p c u"),
-                )
-            hq = work.tile([P, GS], U32, name="hq", align_bytes=64)
-            hs = work.tile([P, GS], U8, name="hs", align_bytes=64)
-            nc.vector.quantize_mx(out=hq[:].bitcast(FP8X4), scales=hs[:], in_=h4_flat)
+                    nc.tensor.transpose(turned[:, c, u, :], pairs[:, P * u : P * (u + 1)], ident[:])
+            copy(
+                h4[g][:].rearrange("p e c t -> p (e c t)").bitcast(F32).rearrange("p (e c u) -> p e c u", e=2, u=2),
+                turned[:].rearrange("p e u c -> p e c u"),
+            )
+
+        def quantise_h(g, tag=None):
+            hq = tile([P, GS], U32, f"hq{g}", tag)
+            hs = tile([P, GS], U8, f"hs{g}")
+            nc.vector.quantize_mx(
+                out=hq[:].bitcast(FP8X4), scales=hs[:], in_=h4[g][:].rearrange("p e c t -> p (e c t)")
+            )
             h_codes[g] = (hq, hs)
 
-        def second_product(g, w2_pair):
+        def second_product(g, banks):
             hq, hs = h_codes[g]
             for n in range(2):
-                y = psum.tile([P, GS], F32, name="bank")
+                y = bank(banks[n], [P, GS], f"y{g}_{n}")
                 y_banks[g, n] = y
                 for c in range(2):
                     cols = slice(C * c, C * (c + 1))
                     nc.tensor.matmul_mx(
                         out=y[:, cols],
-                        lhsT=w2_pair[:, c, 2 * P * n : 2 * P * (n + 1)].bitcast(FP4X4),
+                        lhsT=w2_sb[g][:, c, 2 * P * n : 2 * P * (n + 1)].bitcast(FP4X4),
                         lhsT_scale=s2_sb[:, 2 * g + c, P * n : P * (n + 1)],
                         rhs=hq[:, cols].bitcast(FP8X4),
                         rhs_scale=hs[:, cols],
@@ -243,25 +248,48 @@ def tile_moe_two_glu_sigmoid_kernel(
                         stop=True,
                     )
 
-        def scatter(n, g0, g1, y_sb, gates):
-            for g in range(g0, g1):
-                nc.scalar.copy(y_sb[:, GS * (g - g0) : GS * (g - g0 + 1)], y_banks[g, n][:])
-            nc.vector.tensor_tensor(wins[n][:].indirect(dst_sb[:, GO * g0 : GO * g1]), y_sb[:], gates, MULT)
-            if g1 == G:
-                nc.sync.dma_start(out[P * n : P * (n + 1), :], wins[n][:])
+        def gated(g, tag=None):
+            y_sb[g] = tile([P, GS], F32, f"gated{g}", tag)
+            nc.vector.tensor_tensor(y_sb[g][:], y_banks[g, 0][:], gate_sb[:, GS * g : GS * (g + 1)], MULT)
 
+        def scatter_scalar(g):
+            nc.scalar.activation(wins[0][:].indirect(dst_sb[:, GO * g : GO * (g + 1)]), y_sb[g][:], ACT.Copy)
+
+        def scatter_vector(g0, g1, values):
+            nc.vector.tensor_tensor(
+                wins[1][:].indirect(dst_sb[:, GO * g0 : GO * g1]), values[:], gate_sb[:, GS * g0 : GS * g1], MULT
+            )
+
+        first_layer(0, (0, 1, 2, 3))
         hidden(0)
-        w2_rest = keep.tile([P, E - 2, 2 * N], U8, name="w2_rest", tag="sg0", align_bytes=64)
-        load_words(w2_rest[:], w2_words, 2, E)
         hidden(1)
-        turn_and_quantise(0)
+        first_layer(1, (4, 5, 6, 7))
         hidden(2)
-        second_product(0, w2_first)
-        scatter(0, 0, 1, keep.tile([P, GS], F32, name="y00"), gate_sb[:, 0:GS])
-        turn_and_quantise(1)
-        turn_and_quantise(2)
-        scatter(1, 0, 1, keep.tile([P, GS], F32, name="y01", tag="h5", align_bytes=64), gate_sb[:, 0:GS])
-        second_product(1, w2_rest[:, 0:2, :])
-        second_product(2, w2_rest[:, 2:4, :])
-        for n in range(2):
-            scatter(n, 1, G, keep.tile([P, 2 * GS], F32, name=f"y_rest{n}"), gate_sb[:, GS : G * GS])
+        hidden(3)
+        turn(0, nc.scalar.copy, 0)
+        quantise_h(0)
+        first_layer(2, (1, 2, 3, 4))
+        hidden(4)
+        hidden(5)
+        turn(1, nc.scalar.copy, 1)
+        second_product(0, (5, 6))
+        y_first = tile([P, GS], F32, "y_first")
+        nc.scalar.copy(y_first[:], y_banks[0, 1][:])
+        gated(0)
+        scatter_scalar(0)
+        quantise_h(1, "sg5")
+        turn(2, nc.vector.tensor_copy, 7)
+        second_product(1, (0, 2))
+        gated(1)
+        quantise_h(2)
+        second_product(2, (3, 4))
+        y_rest = tile([P, 2 * GS], F32, "y_rest")
+        nc.scalar.copy(y_rest[:, 0:GS], y_banks[1, 1][:])
+        scatter_scalar(1)
+        gated(2)
+        scatter_vector(0, 1, y_first)
+        nc.scalar.copy(y_rest[:, GS : 2 * GS], y_banks[2, 1][:])
+        scatter_scalar(2)
+        nc.sync.dma_start(out[0:P, :], wins[0][:])
+        scatter_vector(1, G, y_rest)
+        nc.sync.dma_start(out[P : 2 * P, :], wins[1][:])

@@ -178,7 +178,8 @@ def tile_moe_two_glu_sigmoid_kernel(
                 stop=True,
             )
 
-        sg, b_banks, hid, h4, h_codes, y_banks, y_sb = {}, {}, {}, {}, {}, {}, {}
+        sg, hid, h_codes, y_banks, y_sb = {}, {}, {}, {}, {}
+        h4 = [tile([P, 2, C, 4], BF16, f"h4_{g}") for g in range(G)]
 
         def first_product(e, words, scales_sb, b):
             g, c = divmod(e, 2)
@@ -198,30 +199,25 @@ def tile_moe_two_glu_sigmoid_kernel(
         def by_half(sums):
             return sums[:].rearrange("p (q u d) -> p u q d", u=2, d=2)
 
-        def first_layer(g, banks):
-            pair = (2 * g, 2 * g + 1)
-            a = [first_product(e, w1_sb, s1_sb, banks[c]) for c, e in enumerate(pair)]
-            for c, e in enumerate(pair):
-                b_banks[e] = first_product(e, w3_sb, s3_sb, banks[2 + c])
-            for c, e in enumerate(pair):
-                sg[e] = tile([P, 2, P, 2], F32, f"sg{e}")
-                nc.scalar.activation(sg[e][:], by_half(a[c]), ACT.Sigmoid)
+        def sigmoid(e, b):
+            a = first_product(e, w1_sb, s1_sb, b)
+            sg[e] = tile([P, 2, P, 2], F32, f"sg{e}")
+            nc.scalar.activation(sg[e][:], by_half(a), ACT.Sigmoid)
 
-        def hidden(e, tag=None):
-            hid[e] = tile([P, 2, P, 2], BF16, f"h{e}", tag)
-            nc.vector.tensor_tensor(hid[e][:], by_half(b_banks[e]), sg[e][:], MULT)
+        def hidden(e, b):
+            sums = first_product(e, w3_sb, s3_sb, b)
+            hid[e] = tile([P, 2, P, 2], BF16, f"h{e}")
+            nc.vector.tensor_tensor(hid[e][:], by_half(sums), sg[e][:], MULT)
 
-        def turn(g, copy, b):
-            h4[g] = tile([P, 2, C, 4], BF16, f"h4_{g}")
-            turned = bank(b, [P, 2, 2, C], f"turned{g}")
-            for c in range(2):
-                pairs = hid[2 * g + c][:].rearrange("p u q d -> p (u q d)").bitcast(F32)
+        def turn(e0, e1, copy, b):
+            g = e0 // 2
+            turned = bank(b, [P, e1 - e0, 2, C], f"turned{e0}")
+            for e in range(e0, e1):
+                pairs = hid[e][:].rearrange("p u q d -> p (u q d)").bitcast(F32)
                 for u in range(2):
-                    nc.tensor.transpose(turned[:, c, u, :], pairs[:, P * u : P * (u + 1)], ident[:])
-            copy(
-                h4[g][:].rearrange("p e c t -> p (e c t)").bitcast(F32).rearrange("p (e c u) -> p e c u", e=2, u=2),
-                turned[:].rearrange("p e u c -> p e c u"),
-            )
+                    nc.tensor.transpose(turned[:, e - e0, u, :], pairs[:, P * u : P * (u + 1)], ident[:])
+            words = h4[g][:].rearrange("p e c t -> p (e c t)").bitcast(F32).rearrange("p (e c u) -> p e c u", e=2, u=2)
+            copy(words[:, e0 - 2 * g : e1 - 2 * g], turned[:].rearrange("p e u c -> p e c u"))
 
         def quantise_h(g, tag=None):
             hq = tile([P, GS], U32, f"hq{g}", tag)
@@ -260,36 +256,41 @@ def tile_moe_two_glu_sigmoid_kernel(
                 wins[1][:].indirect(dst_sb[:, GO * g0 : GO * g1]), values[:], gate_sb[:, GS * g0 : GS * g1], MULT
             )
 
-        first_layer(0, (0, 1, 2, 3))
-        hidden(0)
-        hidden(1)
-        first_layer(1, (4, 5, 6, 7))
-        hidden(2)
-        hidden(3)
-        turn(0, nc.scalar.copy, 0)
+        sigmoid(0, 0)
+        sigmoid(1, 1)
+        hidden(0, 2)
+        hidden(1, 3)
+        sigmoid(2, 4)
+        sigmoid(3, 5)
+        turn(0, 1, nc.vector.tensor_copy, 0)
+        hidden(2, 6)
+        hidden(3, 7)
+        turn(1, 2, nc.scalar.copy, 1)
         quantise_h(0)
-        first_layer(2, (1, 2, 3, 4))
-        hidden(4)
-        hidden(5)
-        turn(1, nc.scalar.copy, 1)
-        second_product(0, (5, 6))
+        sigmoid(4, 2)
+        sigmoid(5, 3)
+        hidden(4, 4)
+        hidden(5, 5)
+        turn(2, 4, nc.scalar.copy, 2)
+        second_product(0, (6, 0))
         y_first = tile([P, GS], F32, "y_first")
         nc.scalar.copy(y_first[:], y_banks[0, 1][:])
         gated(0)
         scatter_scalar(0)
         quantise_h(1, "sg5")
-        turn(2, nc.vector.tensor_copy, 7)
-        second_product(1, (0, 2))
+        turn(4, 6, nc.vector.tensor_copy, 7)
+        second_product(1, (1, 3))
         gated(1)
         quantise_h(2)
-        second_product(2, (3, 4))
-        y_rest = tile([P, 2 * GS], F32, "y_rest")
-        nc.scalar.copy(y_rest[:, 0:GS], y_banks[1, 1][:])
+        second_product(2, (4, 5))
+        y_rest = [tile([P, GS], F32, f"y_rest{g}") for g in (1, 2)]
+        nc.scalar.copy(y_rest[0][:], y_banks[1, 1][:])
         scatter_scalar(1)
         gated(2)
         scatter_vector(0, 1, y_first)
-        nc.scalar.copy(y_rest[:, GS : 2 * GS], y_banks[2, 1][:])
+        nc.scalar.copy(y_rest[1][:], y_banks[2, 1][:])
         scatter_scalar(2)
         nc.sync.dma_start(out[0:P, :], wins[0][:])
-        scatter_vector(1, G, y_rest)
+        scatter_vector(1, 2, y_rest[0])
+        scatter_vector(2, G, y_rest[1])
         nc.sync.dma_start(out[P : 2 * P, :], wins[1][:])

from contextlib import ExitStack

import concourse.mybir as mybir
from concourse.masks import make_identity

K, T, E, C, H, N = 512, 1536, 6, 128, 512, 256
FLOPS = 2 * E * C * (2 * K * H + H * N)

F32 = mybir.dt.float32
BF16 = mybir.dt.bfloat16
I32 = mybir.dt.int32
U32 = mybir.dt.uint32
U16 = mybir.dt.uint16
U8 = mybir.dt.uint8
FP8X4 = mybir.dt.float8_e4m3fn_x4
FP4X4 = mybir.dt.float4_e2m1fn_x4
ACT = mybir.ActivationFunctionType
MULT = mybir.AluOpType.mult

P = 128
G = E // 2
GS = 2 * C
GO = GS // 16


def tile_moe_two_glu_sigmoid_kernel(
    tc, xT, w1_words, w1_scales, w3_words, w3_scales, w2_words, w2_scales, gate, offs, dst, out
):
    nc = tc.nc
    with ExitStack() as ctx:
        keep = ctx.enter_context(tc.tile_pool(name="keep", bufs=1))
        psum = ctx.enter_context(tc.psum_pool(name="psum", bufs=1))

        def tile(shape, dtype, name, tag=None):
            return keep.tile(shape, dtype, name=name, tag=tag or name, align_bytes=64)

        def bank(b, shape, name):
            return psum.tile(shape, F32, name=name, tag=f"bank{b}")

        offs_sb = tile([P, E * C // 16], U16, "offs_sb")
        dst_sb = tile([P, E * C // 16], U16, "dst_sb")
        ident = tile([P, P], F32, "ident")
        planes = [tile([P, T], F32, f"plane{t}") for t in range(4)]
        wins = [tile([P, T], F32, f"win{n}") for n in range(2)]
        gate_rows = tile([P, C], F32, "gate_rows")
        s1_sb = tile([P, E, H], U8, "s1_sb")
        s3_sb = tile([P, E, H], U8, "s3_sb")
        s2_sb = tile([P, E, N], U8, "s2_sb")
        w1_sb = [tile([P, 2, 2 * H], U8, f"w1_{g}") for g in range(G)]
        w3_sb = [tile([P, 2, 2 * H], U8, f"w3_{g}") for g in range(G)]
        w2_first = tile([P, 2, 2 * N], U8, "w2_first")
        w2_rest = tile([P, E - 2, 2 * N], U8, "w2_rest")
        w2_sb = [w2_first[:], w2_rest[:, 0:2, :], w2_rest[:, 2:4, :]]

        def load_scales(scales_sb, dram):
            flat = scales_sb[:].rearrange("p e i -> p (e i)").bitcast(I32)
            width = scales_sb.shape[2] // 4
            for r in range(4):
                nc.sync.dma_start(
                    out=flat[r:P:32, :].rearrange("q (e i) -> q e i", i=width),
                    in_=dram[:, 0, r:16:4, :].rearrange("e q i -> q e i").bitcast(I32),
                )

        def load_words(words_sb, dram, e0, e1):
            nc.sync.dma_start(
                out=words_sb[:].bitcast(I32),
                in_=dram[e0:e1, 0, :, :].rearrange("e p b -> p e b").bitcast(I32),
            )

        nc.gpsimd.memset(gate_rows[:], 0.0)
        x_rows = xT.rearrange("(p t) j -> p t j", t=4)
        nc.sync.dma_start(out=planes[0][:], in_=x_rows[:, 0, :])
        nc.sync.dma_start(offs_sb[:], offs)
        nc.sync.dma_start(out=gate_rows[0:E, :], in_=gate[0, :].rearrange("(e c) -> e c", c=C))
        for t in range(1, 4):
            nc.sync.dma_start(out=planes[t][:], in_=x_rows[:, t, :])
        load_words(w1_sb[0], w1_words, 0, 2)
        load_scales(s1_sb, w1_scales)
        load_words(w3_sb[0], w3_words, 0, 2)
        load_scales(s3_sb, w3_scales)
        load_words(w1_sb[1], w1_words, 2, 4)
        load_words(w3_sb[1], w3_words, 2, 4)
        load_scales(s2_sb, w2_scales)
        load_words(w1_sb[2], w1_words, 4, 6)
        load_words(w3_sb[2], w3_words, 4, 6)
        load_words(w2_first, w2_words, 0, 2)
        nc.sync.dma_start(dst_sb[:], dst)
        load_words(w2_rest, w2_words, 2, E)

        warm = tile([P, 2], F32, "warm")
        nc.vector.memset(warm[:, 0:1], 0.0)
        nc.scalar.activation(warm[:, 1:2], warm[:, 0:1], ACT.Sigmoid)
        make_identity(nc, ident[:])
        for win in wins:
            nc.vector.memset(win[:], 0.0)

        first = {0: tile([P, 2, GS], BF16, "first01")}
        rest = {t: tile([P, 2, 2 * GS], BF16, f"rest{t}") for t in (0, 2)}
        x4 = [tile([P, GS, 4], BF16, f"x4_{g}") for g in range(G)]
        xq = [tile([P, GS], U32, f"xq_{g}") for g in range(G)]
        xs = [tile([P, GS], U8, f"xs_{g}") for g in range(G)]

        def gather_vector(t, c0=0, c1=2):
            nc.vector.tensor_copy(
                first[t - t % 2][:, t % 2, C * c0 : C * c1], planes[t][:].indirect(offs_sb[:, GO * c0 // 2 : GO * c1 // 2])
            )

        def gather_scalar(t, g0, g1):
            nc.scalar.activation(
                rest[t - t % 2][:, t % 2, GS * (g0 - 1) : GS * (g1 - 1)],
                planes[t][:].indirect(offs_sb[:, GO * g0 : GO * g1]),
                ACT.Copy,
            )

        def weave(copy, g, t, cols=slice(0, GS)):
            rows = first[t][:] if g == 0 else rest[t][:, :, GS * (g - 1) : GS * g]
            copy(x4[g][:, cols, t : t + 2], rows[:, :, cols].rearrange("p t c -> p c t"))

        def quantise_x(g, cols=slice(0, GS)):
            nc.vector.quantize_mx(
                out=xq[g][:, cols].bitcast(FP8X4),
                scales=xs[g][:, cols],
                in_=x4[g][:, cols, :].rearrange("p c t -> p (c t)"),
            )

        gather_vector(0)
        gather_scalar(0, 1, G)
        warm_codes = tile([P, P], U32, "warm_codes")
        warm_scales = tile([P, P], U8, "warm_scales")
        warm_wide = tile([P, H], U8, "warm_wide")
        nc.vector.quantize_mx(out=warm_codes[:].bitcast(FP8X4), scales=warm_scales[:], in_=rest[0][:, 0, :])
        nc.vector.tensor_copy(
            warm_wide[:].bitcast(I32).rearrange("p (r c) -> p r c", r=4),
            warm_scales[:].bitcast(I32).unsqueeze(1).to_broadcast([P, 4, P // 4]),
        )
        gather_vector(1)
        gather_scalar(1, 1, G)
        for g in range(G):
            weave(nc.vector.tensor_copy, g, 0)
        turned_gate = bank(5, [P, P], "turned_gate")
        nc.tensor.transpose(turned_gate[:], gate_rows[:], ident[:])
        gate_col = tile([P, E], F32, "gate_col", "rest0")
        nc.vector.tensor_copy(gate_col[:], turned_gate[:, 0:E])
        first[2] = tile([P, 2, GS], BF16, "first23", "first01")
        gather_vector(2)
        gather_scalar(2, 1, G)
        gather_vector(3, 0, 1)
        gather_vector(3, 1, 2)
        gather_scalar(3, 2, 3)
        gather_scalar(3, 1, 2)
        for c in range(2):
            weave(nc.vector.tensor_copy, 0, 2, slice(C * c, C * (c + 1)))
        for c in range(2):
            quantise_x(0, slice(C * c, C * (c + 1)))
        weave(nc.vector.tensor_copy, 1, 2)
        weave(nc.scalar.copy, 2, 2)
        quantise_x(1)
        quantise_x(2)
        gate_sb = tile([P, E * C], F32, "gate_sb", "x4_0")
        for half in range(2):
            spread = bank(6 + half, [P, 3, C], f"spread{half}")
            for j in range(3):
                e = 3 * half + j
                nc.tensor.transpose(spread[:, j, :], gate_col[:, e : e + 1].to_broadcast([P, P]), ident[:])
            (nc.vector.tensor_copy, nc.scalar.copy)[half](
                gate_sb[:, 3 * C * half : 3 * C * (half + 1)], spread[:].rearrange("p j c -> p (j c)")
            )

        unread = bank(5, [P, H], "unread")
        for width in (H, H // 2):
            nc.tensor.matmul_mx(
                out=unread[:, 0:width],
                lhsT=warm_codes[:].bitcast(FP8X4),
                lhsT_scale=warm_scales[:],
                rhs=w1_sb[0][:, 0, 0 : 2 * width].bitcast(FP4X4),
                rhs_scale=warm_wide[:, 0:width],
                start=True,
                stop=True,
            )

        sg, hid, h_codes, y_banks, y_sb = {}, {}, {}, {}, {}
        h4 = [tile([P, 2, C, 4], BF16, f"h4_{g}") for g in range(G)]

        def first_product(e, words, scales_sb, b):
            g, c = divmod(e, 2)
            cols = slice(C * c, C * (c + 1))
            sums = bank(b, [P, H], f"sums{e}_{b}")
            nc.tensor.matmul_mx(
                out=sums[:],
                lhsT=xq[g][:, cols].bitcast(FP8X4),
                lhsT_scale=xs[g][:, cols],
                rhs=words[g][:, c, :].bitcast(FP4X4),
                rhs_scale=scales_sb[:, e, :],
                start=True,
                stop=True,
            )
            return sums

        def by_half(sums):
            return sums[:].rearrange("p (q u d) -> p u q d", u=2, d=2)

        def sigmoid(e, b):
            a = first_product(e, w1_sb, s1_sb, b)
            sg[e] = tile([P, 2, P, 2], F32, f"sg{e}")
            nc.scalar.activation(sg[e][:], by_half(a), ACT.Sigmoid)

        def hidden(e, b):
            sums = first_product(e, w3_sb, s3_sb, b)
            hid[e] = tile([P, 2, P, 2], BF16, f"h{e}")
            nc.vector.tensor_tensor(hid[e][:], by_half(sums), sg[e][:], MULT)

        def turn(e0, e1, copy, b):
            g = e0 // 2
            turned = bank(b, [P, e1 - e0, 2, C], f"turned{e0}")
            for e in range(e0, e1):
                pairs = hid[e][:].rearrange("p u q d -> p (u q d)").bitcast(F32)
                for u in range(2):
                    nc.tensor.transpose(turned[:, e - e0, u, :], pairs[:, P * u : P * (u + 1)], ident[:])
            words = h4[g][:].rearrange("p e c t -> p (e c t)").bitcast(F32).rearrange("p (e c u) -> p e c u", e=2, u=2)
            copy(words[:, e0 - 2 * g : e1 - 2 * g], turned[:].rearrange("p e u c -> p e c u"))

        def quantise_h(g, tag=None):
            hq = tile([P, GS], U32, f"hq{g}", tag)
            hs = tile([P, GS], U8, f"hs{g}")
            nc.vector.quantize_mx(
                out=hq[:].bitcast(FP8X4), scales=hs[:], in_=h4[g][:].rearrange("p e c t -> p (e c t)")
            )
            h_codes[g] = (hq, hs)

        def second_product(g, banks):
            hq, hs = h_codes[g]
            for n in range(2):
                y = bank(banks[n], [P, GS], f"y{g}_{n}")
                y_banks[g, n] = y
                for c in range(2):
                    cols = slice(C * c, C * (c + 1))
                    nc.tensor.matmul_mx(
                        out=y[:, cols],
                        lhsT=w2_sb[g][:, c, 2 * P * n : 2 * P * (n + 1)].bitcast(FP4X4),
                        lhsT_scale=s2_sb[:, 2 * g + c, P * n : P * (n + 1)],
                        rhs=hq[:, cols].bitcast(FP8X4),
                        rhs_scale=hs[:, cols],
                        start=True,
                        stop=True,
                    )

        def gated(g, tag=None):
            y_sb[g] = tile([P, GS], F32, f"gated{g}", tag)
            nc.vector.tensor_tensor(y_sb[g][:], y_banks[g, 0][:], gate_sb[:, GS * g : GS * (g + 1)], MULT)

        def scatter_scalar(g):
            nc.scalar.activation(wins[0][:].indirect(dst_sb[:, GO * g : GO * (g + 1)]), y_sb[g][:], ACT.Copy)

        def scatter_vector(g0, g1, values):
            nc.vector.tensor_tensor(
                wins[1][:].indirect(dst_sb[:, GO * g0 : GO * g1]), values[:], gate_sb[:, GS * g0 : GS * g1], MULT
            )

        sigmoid(0, 0)
        sigmoid(1, 1)
        hidden(0, 2)
        hidden(1, 3)
        sigmoid(2, 4)
        sigmoid(3, 5)
        turn(0, 1, nc.vector.tensor_copy, 0)
        hidden(2, 6)
        hidden(3, 7)
        turn(1, 2, nc.scalar.copy, 1)
        quantise_h(0)
        sigmoid(4, 2)
        sigmoid(5, 3)
        hidden(4, 4)
        hidden(5, 5)
        turn(2, 4, nc.scalar.copy, 2)
        second_product(0, (6, 0))
        y_first = tile([P, GS], F32, "y_first")
        nc.scalar.copy(y_first[:], y_banks[0, 1][:])
        gated(0)
        scatter_scalar(0)
        quantise_h(1, "sg5")
        turn(4, 6, nc.vector.tensor_copy, 7)
        second_product(1, (1, 3))
        gated(1)
        quantise_h(2)
        second_product(2, (4, 5))
        y_rest = [tile([P, GS], F32, f"y_rest{g}") for g in (1, 2)]
        nc.scalar.copy(y_rest[0][:], y_banks[1, 1][:])
        scatter_scalar(1)
        gated(2)
        scatter_vector(0, 1, y_first)
        nc.scalar.copy(y_rest[1][:], y_banks[2, 1][:])
        scatter_scalar(2)
        nc.sync.dma_start(out[0:P, :], wins[0][:])
        scatter_vector(1, 2, y_rest[0])
        scatter_vector(2, G, y_rest[1])
        nc.sync.dma_start(out[P : 2 * P, :], wins[1][:])
